import numpy as np, ml_dtypes
CORES = [23,119,17,113]
N = 4
BF = ml_dtypes.bfloat16
def gentries(a):
    return np.ascontiguousarray(a.reshape(8, 16, -1).transpose(0, 2, 1)).reshape(8, -1)
def gtable(e):
    e = np.asarray(e); return np.ascontiguousarray(e.reshape(8, -1, 16).transpose(0, 2, 1)).reshape(128, -1).astype(np.int32)
V, G, NB, RO, HP = 1024, 512, 1, 5, 3
H = NB * G
S = V + H
def vals(rng, n):
    p = rng.choice(np.array([0.5, 1.0, 1.0, 2.0]), (N, 8, 1, n)) * rng.choice(np.array([0.7, 1.0, 1.4]), (N, 8, 16, 1))
    return np.minimum((256 * rng.random((N, 8, 16, n)) ** p).astype(np.int64), 255)
def parts(rng):
    m = rng.choice(np.array([2, 4, 16, 16]), (N, 8, 1, V))
    e = np.take_along_axis(rng.integers(0, S, (N, 8, 16, V)), (rng.random((N, 8, 16, V)) * m).astype(np.int64), axis=2)
    share = np.where(rng.random((N, 8, 1, V)) < 0.03125, 1.0, rng.choice(np.array([0.0, 0.0, 0.1, 0.3]), (N, 8, 1, V)))
    e = e + S * (rng.random((N, 8, 16, V)) < share)
    u = rng.integers(0, 16 * V, (N, 8, 16, V)); s = rng.integers(0, V // 4, (N, 8, H))
    h = rng.choice(np.array([200, 600, 1000, 1300, 1600]), (N, 8, RO)) + rng.integers(0, 200, (N, 8, RO))
    return e, u, vals(rng, V), vals(rng, V), vals(rng, S), s, h
def pack(e, u, x, b, y, s, h):
    flat = lambda a: np.ascontiguousarray(a.reshape(N, 128, a.shape[-1]))
    return {"ent": flat(e).astype(np.int32), "usr": flat(u).astype(np.int32), "xa": flat(x).astype(np.float32).astype(BF), "bn": flat(b).astype(np.float32).astype(BF),
            "yc": flat(y).astype(np.float32).astype(BF), "snd": np.stack([gtable(a) for a in s]), "th": np.ascontiguousarray(h).astype(np.int32)}
def setup_inputs(rng):
    return pack(*parts(rng))
def setup_inputs_spread(rng):
    e, u, x, b, y, s, h = parts(rng)
    def uneven(n):
        v = np.minimum((np.exp2(8 * rng.random((N, 8, 1, n))) * rng.random((N, 8, 16, n))).astype(np.int64), 255)
        return np.where(rng.random((N, 8, 1, n)) < 0.5, v, 255 - v)
    src = np.minimum((S * rng.random((N, 8, 16, V)) ** rng.choice(np.array([0.3, 1.0, 3.0]), (N, 8, 1, 1))).astype(np.int64), S - 1)
    e = src + S * (e >= S)
    w = np.minimum((V * rng.random((N, 8, 16, V)) ** rng.choice(np.array([0.5, 1.0, 2.0]), (N, 8, 1, 1))).astype(np.int64), V - 1)
    u = 16 * w + rng.integers(0, 16, (N, 8, 16, V))
    h = np.minimum(np.exp2(12 * rng.random((N, 8, RO))).astype(np.int64) - 1, 4080)
    return pack(e, u, uneven(V), uneven(V), uneven(S), s, h)
def setup_inputs_ends(rng):
    def two(n):
        mode = rng.integers(0, 3, (N, 8, 1, n)); bits = rng.integers(0, 2, (N, 8, 16, n))
        return 255 * np.where(mode == 0, 0, np.where(mode == 1, 1, bits))
    def mix(top, share, other):
        return np.where(rng.random((N, 8, 16, V)) < share, top * rng.integers(0, 2, (N, 8, 16, V)), other)
    x, b, y = two(V), two(V), two(S); v = np.arange(V)
    near = rng.choice(np.array([0, V - 1, V, S - 1, S, S + V - 1, S + V]), (N, 8, 16, V))
    e = mix(2 * S - 1, 0.75, np.where(rng.random((N, 8, 16, V)) < 0.5, near, rng.integers(0, 2 * S, (N, 8, 16, V))))
    u = mix(16 * V - 1, 0.75, rng.integers(0, 16 * V, (N, 8, 16, V)))
    none = v % 8 == 2; one = rng.integers(0, 16, (N, 8, 1, V))
    e = np.where(none, 2 * S - 1, np.where(np.arange(16)[:, None] == one, 0, e))
    top = np.where(np.arange(8) % 2 == 0, 255, 0)[None, :, None]
    x[:, :, :, 0] = top; y[:, :, :, 0] = top; b[:, :, :, 0] = 0; e[:, :, :, 0] = 0
    u[:, :4, 0, 0] = 0; u[:, 4:, 0, 0] = 16 * V - 1
    far = list(range(1, 8)) + list(range(V - 8, V))
    x[:, :, :, far] = 255 - top[..., None]; b[:, :, :, far] = 0; e[:, :, :, far] = 0; u[:, :, 0, far] = 16 * V - 1
    lone = list(range(12, 16)) + list(range(V - 12, V - 8))
    x[:, :, :, lone] = 255 - top[..., None]; e[:, :, :15, lone] = 2 * S - 1; e[:, :, 15, lone] = 0
    still = list(range(8, 12))
    x[:, :, :, still] = top[..., None]; b[:, :, :, still] = 0; e[:, :, :, still] = 0; u[:, :, 0, still] = 0
    s = (V // 4 - 1) * rng.integers(0, 2, (N, 8, H))
    h = 4080 * rng.integers(0, 2, (N, 8, RO)); h[:, 0, 0] = 0; h[:, 1, 0] = 0; h[:, 6, 0] = 4080; h[:, 7, 0] = 4080; h[N - 1, :, 1] = 4080
    return pack(e, u, x, b, y, s, h)
def setup_inputs_corners(rng):
    e, u, x, b, y, s, h = parts(rng); v = np.arange(V)
    src = rng.integers(0, S, (N, 8, 16, V)); src[:, 3] = v; src[:, 5] = rng.integers(V, S, (N, 16, V))
    src[:, 6] = rng.choice(np.array([0, V - 1, V, S - 1]), (N, 16, V))
    cl = rng.choice(np.array([0, 1, 2, 15, 16]), (N, 8, 1, V)); cl[:, 5] = 16
    o = np.argsort(rng.random((N, 8, 16, V)), axis=2); o[:, 0] = np.arange(15, -1, -1)[:, None]; o[:, 7] = np.arange(16)[:, None]
    gone = o >= cl; gone[:, 4, 15] = True
    q = rng.integers(0, 16, (N, 8, 16, V))
    u[:, 1] = 16 * np.where(v < V // 2, v, v ^ 1) + q[:, 1]; u[:, 2] = 16 * ((v + 1) % V) + q[:, 2]
    u[:, 3] = 16 * rng.choice(np.array([0, V - 1]), (N, 16, V)) + q[:, 3]; u[:, 4] = 16 * (u[:, 4] >> 4) + 15
    e = src + S * gone
    for a in range(N):
        turn = np.roll(np.arange(8), a); e[a] = e[a][turn]; u[a] = u[a][turn]
    e[1, :, :, 2::4] = e[1, :, :, 2::4] % S + S
    s[:, ::2] = rng.choice(np.array([0, V // 4 - 1]), (N, 4, H))
    h = rng.choice(np.array([0, 1, 300, 1000, 1400, 4079, 4080]), (N, 8, RO))
    return pack(e, u, x, b, y, s, h)
def setup_inputs_limits(rng):
    e, u, x, b, y, s, h = parts(rng); m = V // 4; a = np.arange(N)[:, None]; g = np.arange(8)[None, :]; k = np.arange(16)[:, None]; p = rng.permutation(N)
    base = np.where((a + g) % 2 == 0, rng.integers(2048, 3824, (N, 8)), rng.integers(64, 1700, (N, 8)))
    eff = base[..., None] + np.argsort(rng.random((N, 8, m)), axis=2)
    d = (eff[:, :, None] + np.argsort(rng.random((N, 8, 16, m)), axis=2)) // 16
    mv = (rng.random((N, 8, 8, m)) * (np.minimum(255 - d[:, :, :8], d[:, :, 8:]) + 1)).astype(np.int64)
    d = np.concatenate([d[:, :, :8] + mv, d[:, :, 8:] - mv], axis=2)
    fv = (rng.random(d.shape) * (np.minimum(128, 255 - d) + 1)).astype(np.int64)
    x[..., 3::4] = np.where((fv >= d) & (rng.random(d.shape) < 0.5), fv - d, fv + d)
    b[..., 3::4] = np.where((fv < 128) & (rng.random(d.shape) < 0.5), 127 - fv, 127 + fv)
    w = 4 * np.argsort(rng.random((N, 8, 4, m)), axis=3) + 3
    u = 16 * w.transpose(0, 1, 3, 2).reshape(N, 8, 1, V) + rng.integers(8, 16, (N, 8, 16, V))
    e = np.where(k == rng.integers(0, 16, (N, 8, 1, V)), e % S, e)
    o = np.argsort(rng.random((N, 8, S)), axis=2); lo, hi = o[..., 0], o[..., 1]
    y[a, g, :, lo] = 0; y[a, g, :, hi] = 255; lo = lo[..., None]; hi = hi[..., None]
    c = rng.integers(0, 2, (N, 8, m)) == 1
    e[..., 3::4] = e[..., 3::4] % S + S * (k < 8)
    e[:, :, 0, 3::4] = S + np.where(c, lo, hi); e[:, :, 7, 3::4] = S + np.where(c, hi, lo)
    h = base[..., None] + rng.integers(32, m - 64, (N, 8, RO))
    h = h - (h & 15) + rng.choice(np.array([0, 1, 2, 3, 4, 5, 10, 11, 12, 13, 14, 15]), h.shape)
    h[p[:2], :, 0] = 4080; h[p[2:], rng.integers(0, 8, N - 2), 0] = 4080; h[p[1], :, 1] = 0
    few = 4 * rng.permutation(m)[:int(rng.integers(1, 32))]; ez = e[p[1], int(rng.integers(0, 8))]
    ez[:, few] = ez[:, few] % S + S
    e[p[1], ::2, :, 1::4] = e[p[1], ::2, :, 1::4] % S + S
    return pack(e, u, x, b, y, s, h)
def setup_inputs_ties(rng):
    e, u, x, b, y, s, h = parts(rng)
    base = rng.choice(np.array([0, 100, 252]), (N, 8, 1, 1)); base[:, 0] = 252; base[:, 7] = 0
    x = base + rng.integers(0, 4, (N, 8, 16, V)); y = base + rng.integers(0, 4, (N, 8, 16, S)); b = rng.integers(0, 4, (N, 8, 16, V))
    x[:, :, :, 1::4] = x[:, :, :, 0::4]; x[:, :, :, 3::4] = x[:, :, :, 2::4]
    h = rng.integers(0, 40, (N, 8, RO))
    return pack(e, u, x, b, y, s, h)
def check_inputs(d):
    bad = []
    for k, lo, hi in (("ent", 0, 2 * S - 1), ("usr", 0, 16 * V - 1), ("xa", 0, 255), ("bn", 0, 255), ("yc", 0, 255), ("snd", 0, V // 4 - 1), ("th", 0, 4080)):
        v = np.asarray(d[k]).astype(np.float64)
        if not np.all((v >= lo) & (v <= hi)): bad.append("range of " + k)
        elif np.any(v != np.floor(v)): bad.append("whole numbers of " + k)
    return bad
def mid(a, b):
    return np.abs(((np.maximum.reduce(a, axis=3) + np.minimum.reduce(a, axis=3)) >> 1) - b)
def nodes(a, dtype):
    return np.ascontiguousarray(np.asarray(a).astype(np.float32).astype(dtype).reshape(N, 8, 16, -1).transpose(0, 1, 3, 2))
def reference(ent, usr, xa, bn, yc, snd, th):
    e, u = nodes(ent, np.int64), nodes(usr, np.int64); x, b, y = nodes(xa, np.int32), nodes(bn, np.int32), nodes(yc, np.int32)
    sl = np.stack([gentries(a) for a in snd]).astype(np.int64).reshape(N, 8, NB, 4, G // 4) * 4 + np.arange(4)[:, None]
    sl = sl.reshape(N, 8, NB, G); hh = th.astype(np.int64)
    r3 = np.arange(N)[:, None, None]; g3 = np.arange(8)[None, :, None]; r4 = r3[..., None]; g4 = g3[..., None]; sixteen = np.arange(16)
    gone = np.zeros(N, np.int64)
    for t in range(RO):
        w = [x]
        for n in range(1, NB + 1):
            q = (np.arange(N) + n) % N
            w.append(x[q][r3, g3, sl[q, :, n - 1]])
        w = np.concatenate(w + [y], axis=2)
        own = np.arange(t % 4, V, 4)
        eo = e[:, :, own]; xo = x[:, :, own]; bo = b[:, :, own]
        src = w[r4, g4, eo]
        score = np.add.reduce(np.abs(src - xo[:, :, :, None]), axis=4); clean = eo < S; some = np.any(clean, axis=3)
        k = np.argmin(np.where(clean, score, 9999), axis=3)
        hit = (sixteen == k[..., None]) & some[..., None]
        ek = np.take_along_axis(eo, k[..., None], 3)[..., 0]
        cv = w[r3, g3, np.where(some, ek + S, 0)]
        f0 = mid(src, bo); z = mid(np.where(hit[..., None], cv[:, :, :, None], src), bo); z0 = z
        c = np.broadcast_to(own, some.shape); dead = np.zeros(some.shape, bool)
        for hop in range(HP):
            p = u[r3, g3, c, np.add.reduce(z, axis=3) & 15]
            c = p >> 4; at = sixteen == (p & 15)[..., None]; ew = e[r3, g3, c]
            dead = dead | np.any(at & (ew >= S), axis=3)
            z = mid(np.where(at[..., None], z[:, :, :, None], w[r4, g4, ew]), b[r3, g3, c])
        D = np.where(dead, 0, np.add.reduce(np.abs(z - x[r3, g3, c]), axis=3))
        stay = some & (D <= hh[:, :, t][..., None] + (gone & 31)[:, None, None])
        e[:, :, own] = np.where(stay[..., None] & hit, eo + S, eo)
        x[:, :, own] = np.where(stay[..., None], z0, f0)
        gone = np.add.reduce(stay.astype(np.int64), axis=(1, 2))
    return {"ye": np.ascontiguousarray(e.transpose(0, 1, 3, 2)).reshape(N, 128, V).astype(np.float32), "yx": np.ascontiguousarray(x.transpose(0, 1, 3, 2)).reshape(N, 128, V).astype(np.float32).astype(BF)}

@@ -1,0 +1,476 @@
+from concourse.mybir import dt, AluOpType, AxisListType, ActivationFunctionType
+A = AluOpType
+F = ActivationFunctionType
+
+V, H, S = 1024, 512, 1536
+NS, M = 2, 128
+CH = 2
+CN = M // CH
+RO, HP = 5, 3
+X0, G0, Y0, ZB = 128, 1152, 1664, 3200
+CMOD = 201326592.0
+CINT = 8388608.0
+HB = 1536.0
+QOFF = 196608.0 - 1024.0 * HB
+
+SCRATCH = {
+    "W": ("sbuf", [128, 3328], "bfloat16"),
+    "enti": ("sbuf", [128, 1024], "int32"),
+    "E": ("sbuf", [128, 1024], "float32"),
+    "usri": ("sbuf", [128, 1024], "int32"),
+    "Uw": ("sbuf", [128, 1024], "int32"),
+    "Uq": ("sbuf", [128, 1024], "int32"),
+    "BN": ("sbuf", [128, 1024], "bfloat16"),
+    "sndi": ("sbuf", [128, 32], "int32"),
+    "snd16": ("sbuf", [128, 32], "uint16"),
+    "gi16": ("sbuf", [128, 32], "uint16"),
+    "thi": ("sbuf", [8, 5], "int32"),
+    "thf": ("sbuf", [8, 5], "float32"),
+    "thr": ("sbuf", [128, 8], "float32"),
+    "XGi": ("sbuf", [128, 512], "bfloat16"),
+    "XN": ("sbuf", [128, 256], "bfloat16"),
+    "rs": ("sbuf", [128, 2], "float32"),
+    "rsum": ("sbuf", [128, 8], "float32"),
+    "rint": ("sbuf", [128, 16], "int32"),
+    "rand": ("sbuf", [128, 16], "int32"),
+    "junk": ("sbuf", [128, 256], "bfloat16"),
+    "c_one": ("sbuf", [128, 128], "float32"),
+    "c_if": ("sbuf", [128, 128], "float32"),
+    "c_t1": ("sbuf", [128, 128], "float32"),
+    "c_bof": ("sbuf", [128, 128], "float32"),
+    "c_os": ("sbuf", [128, 128], "float32"),
+    "c_pi": ("sbuf", [128, 1], "int32"),
+    "c_ki": ("sbuf", [128, 1], "int32"),
+    "kcol": ("sbuf", [128, 1], "float32"),
+    "nkcol": ("sbuf", [128, 1], "float32"),
+    "k16": ("sbuf", [128, 1], "float32"),
+    "c_cl": ("sbuf", [128, 8], "int32"),
+    "clist": ("sbuf", [128, 8], "uint16"),
+    "c_nb": ("sbuf", [128, 8], "int32"),
+    "nbase": ("sbuf", [128, 8], "bfloat16"),
+    "zix0": ("sbuf", [128, 128], "float32"),
+    "zix1": ("sbuf", [128, 128], "float32"),
+    "ones": ("sbuf", [128, 128], "bfloat16"),
+    "I": ("sbuf", [128, 128], "bfloat16"),
+    "nI": ("sbuf", [128, 128], "bfloat16"),
+    "n2I": ("sbuf", [128, 128], "bfloat16"),
+    "bigI": ("sbuf", [128, 128], "bfloat16"),
+    "NK": ("sbuf", [128, 128], "bfloat16"),
+    "KD": ("sbuf", [128, 128], "bfloat16"),
+    "BO": ("sbuf", [128, 128], "bfloat16"),
+    "BD": ("sbuf", [128, 128], "bfloat16"),
+    "BH": ("sbuf", [128, 128], "bfloat16"),
+    "BG": ("sbuf", [128, 8], "bfloat16"),
+    "BOh": ("sbuf", [128, 128], "float16"),
+    "WR": ("sbuf", [128, 2048], "float16"),
+    "mk_mx": ("sbuf", [128, 1024], "bfloat16"),
+    "mk_mn": ("sbuf", [128, 1024], "bfloat16"),
+    "mk_ky": ("sbuf", [128, 128], "float32"),
+    "ex8": ("sbuf", [8, 128], "float32"),
+}
+SCRATCH["XG"] = ("sbuf", [128, 512], "bfloat16")
+SCRATCH["gl"] = ("sbuf", [128, 512], "bfloat16")
+for _s in range(NS):
+    for _n, _w, _d in (("e16", 128, "uint16"), ("cm", 128, "bfloat16"), ("src", 2048, "bfloat16"), ("ab", 2048, "bfloat16"),
+                       ("mx", 2048, "bfloat16"), ("mn", 2048, "bfloat16"), ("key", 128, "float32"), ("r1", 128, "float32"),
+                       ("hit", 128, "bfloat16"), ("hs", 128, "bfloat16"), ("pp", 256, "float16"), ("lst", 16, "uint16"),
+                       ("ta", 8, "uint16"), ("tb", 8, "uint16"), ("yv", 128, "bfloat16"), ("fa", 128, "float32"),
+                       ("f0", 128, "bfloat16"), ("d0", 128, "bfloat16"), ("r16", 128, "bfloat16"), ("msk", 128, "bfloat16"),
+                       ("tt", 128, "float32"), ("cc", 128, "float32"), ("ev", 128, "float32"), ("v1", 128, "float32"),
+                       ("dm", 384, "bfloat16"), ("bg", 128, "bfloat16"),
+                       ("xw", 128, "bfloat16"), ("da", 128, "bfloat16"), ("st", 128, "bfloat16"), ("sd", 128, "bfloat16"),
+                       ("eu", 128, "bfloat16")):
+        SCRATCH["%s_%d" % (_n, _s)] = ("sbuf", [128, _w], _d)
+for _b in range(8):
+    SCRATCH["bk%d" % _b] = ("psum", [128, 512], "float32")
+
+SEMAPHORES = ["qV", "qS", "qP", "qG", "gini", "lini"] + ["ga%d" % t for t in range(4)] + ["ls%d" % t for t in range(4)] + ["d%d" % i for i in range(24)]
+
+CY = 0.83
+
+
+def program(T, topo, core):
+    ops = []
+    c_g = 1.5 * CY
+
+    def op(eng, cost, reads, writes, fn, bank=None, sem=None):
+        ops.append(dict(eng=eng, cost=cost, r=reads.split(), w=writes.split(), fn=fn, bank=bank, sem=sem))
+
+    def vec(n, half=False, two=False):
+        return 60 + max(64, n * (0.5 if half else 2 if two else 1)) * CY
+
+    def vgat(n):
+        return 60 + n * c_g
+
+    def act(n):
+        return 90 + n * CY
+
+    def mm(cy):
+        return 60 + cy * CY
+
+    B = lambda n, s: T["%s_%d" % (n, s)]
+    rank = T.rank_of(core)
+    dst = T.cores[(rank - 1) % 4]
+    rid, pid = topo.addr(dst)[0], topo.addr(dst)[1]
+    mask = topo.mask(core, dst)
+    W = T.W
+
+    dn = [0]
+
+    def dma(eng, cost, reads, writes, out, in_):
+        name = "d%d" % dn[0]
+        dn[0] += 1
+        op(eng, cost, reads, writes, (lambda q, out=out, in_=in_: q.dma_start(out, in_)), sem=(name, 16))
+
+    dma("D", 3000, "", "sndi", T.sndi[:], T.snd[:])
+    dma("D", 3500, "", "Wx", W[:, X0:G0], T.xa[:])
+    dma("D", 5000, "", "enti", T.enti[:], T.ent[:])
+    dma("D", 6500, "", "Wy", W[:, Y0:ZB], T.yc[:])
+    dma("D", 8000, "", "BN", T.BN[:], T.bn[:])
+    dma("D", 9500, "", "usri", T.usri[:], T.usr[:])
+    dma("D", 10000, "", "thi", T.thi[:], T.th[:])
+
+    for c in range(4):
+        op("V", vec(8), "sndi", "gi16", lambda q, c=c: q.tensor_scalar(T.gi16[:, 8 * c:8 * c + 8], T.sndi[:, 8 * c:8 * c + 8], 4, c, A.mult, A.add))
+    op("V", vgat(512), "gi16 Wx", "XGi", lambda q: q.tensor_copy(T.XGi[:], W[:, X0:G0].indirect(T.gi16[:])))
+    op("R", 2000, "XGi", "sent", lambda q: q.remote_dma(T.W[:, G0:Y0], T.XGi[:], T.sem["gini"], T.sem["lini"], pid, rid, mask), sem=("lini", bin(mask).count("1")))
+    op("X", 5000, "sent", "Wg", None, sem=("gini", bin(mask).count("1")))
+    op("V", vec(32), "sndi", "snd16", lambda q: q.tensor_copy(T.snd16[:], T.sndi[:]))
+
+    op("V", vec(128), "", "c_one", lambda q: q.memset(T.c_one[:], 1.0))
+    op("V", vec(128), "", "ones", lambda q: q.memset(T.ones[:], 1.0))
+    op("V", vec(128), "", "c_os", lambda q: q.memset(T.c_os[:], 0.0625))
+    op("V", vec(128), "", "za0", lambda q: q.memset(W[:, 0:X0], 0.0))
+    op("V", vec(128), "", "za1", lambda q: q.memset(W[:, ZB:ZB + 128], 0.0))
+    op("V", vec(1024, True), "", "mk_mx", lambda q: q.memset(T.mk_mx[:], 255.0))
+    op("V", vec(64), "", "mk_mx", lambda q: q.memset(T.mk_mx[:, 0:1024:16], 0.0))
+    op("V", vec(1024, True), "", "mk_mn", lambda q: q.memset(T.mk_mn[:], 0.0))
+    op("V", vec(64), "", "mk_mn", lambda q: q.memset(T.mk_mn[:, 0:1024:16], 255.0))
+    op("V", vec(128), "", "mk_ky", lambda q: q.memset(T.mk_ky[:], 0.0))
+    op("V", vec(64), "", "mk_ky", lambda q: q.memset(T.mk_ky[:, 0:128:16], 131071.0))
+    op("G", 400, "c_one", "c_if", lambda q: q.affine_select(T.c_if[:], T.c_one[:], [[-1, 128]], A.is_equal, 0.0, 0, 1))
+    op("G", 400, "c_one", "c_t1", lambda q: q.affine_select(T.c_t1[:], T.c_one[:], [[-16, 8], [0, 16]], A.is_ge, 0.0, 0, 1))
+    op("G", 400, "c_t1", "c_bof", lambda q: q.affine_select(T.c_bof[:], T.c_t1[:], [[16, 8], [0, 16]], A.is_ge, 0.0, 15, -1))
+    op("G", 200, "", "c_pi", lambda q: q.iota(T.c_pi[:], [[0, 1]], 0, 1))
+    op("G", 200, "", "c_cl", lambda q: q.iota(T.c_cl[:], [[16, 8]], 15, 0))
+    op("G", 200, "", "c_nb", lambda q: q.iota(T.c_nb[:], [[256, 8]], 0, 0))
+    op("G", 400, "", "zix0", lambda q: q.iota(T.zix0[:], [[1, 128]], -128, 0, allow_small_or_imprecise_dtypes=True))
+    op("G", 400, "", "zix1", lambda q: q.iota(T.zix1[:], [[1, 128]], 3072, 0, allow_small_or_imprecise_dtypes=True))
+    op("G", 400, "c_one", "ex8t", lambda q: q.affine_select(T.ex8[:], T.c_one[0:8, :], [[-1, 8], [0, 16]], A.is_equal, 0.0, 0, 1))
+    op("V", vec(1), "c_pi", "c_ki", lambda q: q.tensor_scalar(T.c_ki[:], T.c_pi[:], 15, None, A.bitwise_and))
+    op("V", vec(1), "c_ki", "kcol", lambda q: q.tensor_copy(T.kcol[:], T.c_ki[:]))
+    op("V", vec(1), "kcol", "nkcol", lambda q: q.tensor_scalar(T.nkcol[:], T.kcol[:], -1.0, None, A.mult))
+    op("V", vec(1), "kcol", "k16", lambda q: q.tensor_scalar(T.k16[:], T.kcol[:], 16.0, None, A.mult))
+    op("V", vec(8), "c_cl", "clist", lambda q: q.tensor_copy(T.clist[:], T.c_cl[:]))
+    op("V", vec(8), "c_nb k16", "nbase", lambda q: q.tensor_scalar(T.nbase[:], T.c_nb[:], T.k16[:], None, A.add))
+    op("V", vec(128), "c_if", "I", lambda q: q.tensor_copy(T.I[:], T.c_if[:]))
+    op("V", vec(128), "c_if", "nI", lambda q: q.tensor_scalar(T.nI[:], T.c_if[:], -1.0, None, A.mult))
+    op("V", vec(128), "c_if", "n2I", lambda q: q.tensor_scalar(T.n2I[:], T.c_if[:], -2.0, None, A.mult))
+    op("V", vec(128), "c_if", "bigI", lambda q: q.tensor_scalar(T.bigI[:], T.c_if[:], 131072.0, None, A.mult))
+    op("V", vec(128), "c_if nkcol", "NK", lambda q: q.tensor_scalar(T.NK[:], T.c_if[:], T.nkcol[:], None, A.mult))
+    op("V", vec(128), "c_if kcol", "KD", lambda q: q.tensor_scalar(T.KD[:], T.c_if[:], T.kcol[:], None, A.mult))
+    op("V", vec(128), "c_bof", "BO", lambda q: q.tensor_copy(T.BO[:], T.c_bof[:]))
+    op("V", vec(128), "c_bof", "BD", lambda q: q.tensor_scalar(T.BD[:], T.c_bof[:], -4096.0, None, A.mult))
+    op("V", vec(128), "c_bof", "BH", lambda q: q.tensor_scalar(T.BH[:], T.c_bof[:], -1024.0, None, A.mult))
+    op("V", vec(8), "c_bof", "BG", lambda q: q.tensor_scalar(T.BG[:], T.c_bof[:, 0:128:16], 16.0, None, A.mult))
+    op("V", vec(128), "c_bof", "BOh", lambda q: q.tensor_copy(T.BOh[:], T.c_bof[:]))
+    for h in range(2):
+        op("V", vec(1024, True), "mk_mn", "WR", lambda q, h=h: q.tensor_scalar(T.WR[:, 1024 * h:1024 * h + 1024], T.mk_mn[:], 0.0, None, A.mult))
+    for r in range(16):
+        op("V", vec(8), "c_bof", "WR", lambda q, r=r: q.tensor_copy(T.WR[:, 128 * r + r:128 * r + 128:16], T.c_bof[:, 0:128:16]))
+    op("V", vec(5), "thi", "thf", lambda q: q.tensor_copy(T.thf[:], T.thi[:]))
+    op("P", mm(512), "thf ex8t", "ps_th", lambda q: q.matmul(T.bk0[:, 0:5], T.ex8[:], T.thf[:], True, True), bank=0)
+    op("V", vec(5), "ps_th", "thb thr0", lambda q: q.tensor_scalar(T.thr[:, 0:5], T.bk0[:, 0:5], QOFF, None, A.add), bank=0)
+
+    ecls = lambda s, cl: "E%d%d" % (s, cl)
+    eall = " ".join(ecls(s, cl) for s in range(NS) for cl in range(4))
+    for cl in range(4):
+        for s in range(NS):
+            sl = slice(512 * s + cl, 512 * s + 512, 4)
+            op("V", vec(128), "enti", ecls(s, cl), lambda q, sl=sl: q.tensor_copy(T.E[:, sl], T.enti[:, sl]))
+    op("V", vec(1024), "usri", "Uq", lambda q: q.tensor_scalar(T.Uq[:], T.usri[:], 15, None, A.bitwise_and))
+    op("V", vec(1024), "usri", "Uw", lambda q: q.tensor_scalar(T.Uw[:], T.usri[:], 4, None, A.arith_shift_right))
+
+    def mms(q, lst):
+        r = None
+        for a in lst:
+            r = q.matmul(*a)
+        return r
+
+    zcol = (slice(0, 128), slice(ZB, ZB + 128))
+    wins = (slice(0, ZB), slice(X0, ZB + 128))
+    shift = (float(X0), 0.0)
+
+    def bkA(s): return 2 * s
+    def bkB(s): return 2 * s + 1
+    PA = (T.bk0, T.bk2)
+    PB = (T.bk1, T.bk3)
+    PJ = (T.bk4, T.bk5, T.bk6, T.bk7)
+
+    def gather(s):
+        z = "za%d" % s
+        for c in range(CH):
+            op("S", 90 + 16 * CN * c_g, "e16_%d Wx Wg Wy %s" % (s, z), "src%d%d" % (s, c),
+               lambda q, s=s, c=c: q.activation(B("src", s)[:, 16 * CN * c:16 * CN * (c + 1)], W[:, wins[s]].indirect(B("e16", s)[:, CN * c:CN * (c + 1)]), F.Copy))
+
+    def scans(s):
+        for c in range(CH):
+            sl = slice(16 * CN * c, 16 * CN * (c + 1))
+            op("V", vec(16 * CN, True), "src%d%d mk_mx" % (s, c), "mx%d%d" % (s, c),
+               lambda q, s=s, sl=sl: q.tensor_tensor_scan(B("mx", s)[:, sl], T.mk_mx[:, 0:16 * CN], B("src", s)[:, sl], 0.0, A.min, A.max))
+            op("V", vec(16 * CN, True), "src%d%d mk_mn" % (s, c), "mn%d%d" % (s, c),
+               lambda q, s=s, sl=sl: q.tensor_tensor_scan(B("mn", s)[:, sl], T.mk_mn[:, 0:16 * CN], B("src", s)[:, sl], 255.0, A.max, A.min))
+
+    def half(s, bsrc, btok, out, otok):
+        rd = " ".join("mx%d%d mn%d%d" % (s, c, s, c) for c in range(CH))
+        op("P", mm(384), rd + " I n2I " + btok, "h%d" % s, lambda q, s=s: mms(q, [
+            (PA[s][:, 0:128], T.n2I[:], bsrc, True, False),
+            (PA[s][:, 0:128], T.I[:], B("mx", s)[:, 15:2048:16], False, False),
+            (PA[s][:, 0:128], T.I[:], B("mn", s)[:, 15:2048:16], False, True)]), bank=bkA(s))
+        op("S", act(128), "h%d" % s, "fa%d" % s, lambda q, s=s: q.activation(B("fa", s)[:], PA[s][:, 0:128], F.Abs, bias=-0.25, scale=0.5), bank=bkA(s))
+        op("V", vec(128), "fa%d" % s, otok, lambda q, s=s: q.tensor_scalar(out, B("fa", s)[:], CINT, CINT, A.add, A.subtract))
+
+    def one_round(t):
+        cl = t % 4
+        csl = [slice(512 * s + cl, 512 * s + 512, 4) for s in range(NS)]
+        xsl = [slice(X0 + 512 * s + cl, X0 + 512 * s + 512, 4) for s in range(NS)]
+        for s in range(NS):
+            ec = ecls(s, cl)
+            op("V", vec(128), ec, "e16_%d" % s, lambda q, s=s: q.tensor_scalar(B("e16", s)[:], T.E[:, csl[s]], shift[s], None, A.add))
+            op("V", vec(128), ec, "cm%d" % s, lambda q, s=s: q.tensor_scalar(B("cm", s)[:], T.E[:, csl[s]], float(S), None, A.is_ge))
+            gather(s)
+            sr = " ".join("src%d%d" % (s, c) for c in range(CH))
+            op("P", mm(256), "ones KD cm%d bigI" % s, "ky%d" % s, lambda q, s=s: mms(q, [
+                (PB[s][:, 0:128], T.ones[:], T.KD[:], True, False),
+                (PB[s][:, 0:128], B("cm", s)[:], T.bigI[:], False, False)]), bank=bkB(s))
+            for b in range(4):
+                op("P", mm(1024), sr + " I nI Wx", "j%d" % b, lambda q, s=s, b=b: mms(q, [
+                    a for k in range(4) for a in (
+                        (PJ[b][:, 128 * k:128 * k + 128], T.I[:], B("src", s)[:, 4 * b + k:2048:16], True, False),
+                        (PJ[b][:, 128 * k:128 * k + 128], T.nI[:], W[:, xsl[s]], False, True))]), bank=4 + b)
+                op("S", act(512), "j%d" % b, "ab%d%d" % (s, b), lambda q, s=s, b=b: q.activation(B("ab", s)[:, 512 * b:512 * b + 512], PJ[b][:], F.Abs), bank=4 + b)
+                op("P", mm(256), "ab%d%d BG" % (s, b), "ky%d" % s, lambda q, s=s, b=b: mms(q, [
+                    (PB[s][:, k:128:16], B("ab", s)[:, 128 * k:128 * k + 128], T.BG[:], False, k == 15) for k in range(4 * b, 4 * b + 4)]), bank=bkB(s))
+            scans(s)
+            half(s, T.BN[:, csl[s]], "BN", B("f0", s)[:], "f0%d" % s)
+            op("S", act(128), "ky%d" % s, "key%d" % s, lambda q, s=s: q.activation(B("key", s)[:], PB[s][:, 0:128], F.Copy), bank=bkB(s))
+            op("V", vec(128), "key%d mk_ky" % s, "r1%d" % s, lambda q, s=s: q.tensor_tensor_scan(B("r1", s)[:], T.mk_ky[:], B("key", s)[:], 131071.0, A.max, A.min))
+            op("V", vgat(128), "r1%d key%d clist" % (s, s), "hit%d" % s, lambda q, s=s: q.tensor_tensor(B("hit", s)[:], B("r1", s)[:].indirect(T.clist[:]), B("key", s)[:], A.is_equal))
+            op("P", mm(128), "hit%d I" % s, "ht%d" % s, lambda q, s=s: q.matmul(PA[s][:, 0:128], B("hit", s)[:], T.I[:], True, True), bank=bkA(s))
+            op("V", vec(128), "ht%d %s" % (s, ec), "pw%d" % s, lambda q, s=s: q.tensor_tensor(B("pp", s)[:, 0:128], PA[s][:, 0:128], T.E[:, csl[s]], A.mult), bank=bkA(s))
+            op("V", vec(128), "ht%d kcol" % s, "pq%d" % s, lambda q, s=s: q.tensor_scalar(B("pp", s)[:, 128:256], PA[s][:, 0:128], T.kcol[:], None, A.mult), bank=bkA(s))
+            op("S", act(128), "ht%d" % s, "hs%d" % s, lambda q, s=s: q.activation(B("hs", s)[:], PA[s][:, 0:128], F.Copy, scale=HB), bank=bkA(s))
+            op("P", mm(17 * 64), "pw%d pq%d WR I nbase" % (s, s), "wp%d" % s, lambda q, s=s: mms(q, [
+                (PB[s][:, 0:16], T.WR[:, 128 * r:128 * r + 128], B("pp", s)[:, r:256:16], r == 0, False) for r in range(16)] + [
+                (PB[s][:, 8:16], T.I[:], T.nbase[:], False, True)]), bank=bkB(s))
+            op("V", vec(16), "wp%d" % s, "lst%d" % s, lambda q, s=s: q.tensor_copy(B("lst", s)[:], PB[s][:, 0:16]), bank=bkB(s))
+            op("V", vgat(128), "lst%d Wy" % s, "yv%d" % s, lambda q, s=s: q.tensor_copy(B("yv", s)[:], W[:, Y0:ZB].indirect(B("lst", s)[:, 0:8])))
+            allsrc = " ".join("src%d%d" % (s, c) for c in range(CH))
+            op("V", 60 + 128 * 3.5 * CY, "lst%d yv%d" % (s, s), allsrc, lambda q, s=s: q.tensor_copy(B("src", s)[:].indirect(B("lst", s)[:, 8:16]), B("yv", s)[:]))
+            scans(s)
+            half(s, T.BN[:, csl[s]], "BN", W[:, zcol[s]], "za%d" % s)
+            op("V", vec(128, two=True), "za%d f0%d" % (s, s), "d0%d" % s, lambda q, s=s: q.tensor_tensor(B("d0", s)[:], W[:, zcol[s]], B("f0", s)[:], A.subtract))
+        for h in range(HP):
+            for s in range(NS):
+                z = "za%d" % s
+                nt, ct = ("ta", "tb")[h % 2], ("tb", "ta")[h % 2]
+                op("P", mm(256), z + " NK ones BO", "s%d" % s, lambda q, s=s: mms(q, [
+                    (PA[s][:, 0:128], T.NK[:], T.ones[:], True, False),
+                    (PA[s][:, 0:128], T.BO[:], W[:, zcol[s]], False, True)]), bank=bkA(s))
+                op("V", vec(128), "s%d" % s, "r16%d" % s, lambda q, s=s: q.tensor_scalar(B("r16", s)[:], PA[s][:, 0:128], CMOD, CMOD, A.add, A.subtract), bank=bkA(s))
+                op("V", vec(128), "s%d r16%d" % (s, s), "msk%d" % s, lambda q, s=s: q.tensor_tensor(B("msk", s)[:], PA[s][:, 0:128], B("r16", s)[:], A.is_equal), bank=bkA(s))
+                for nm, tab, lo in (("pq", T.Uq, 128), ("pw", T.Uw, 0)):
+                    if h == 0:
+                        op("V", vec(128, two=True), "msk%d U%s" % (s, nm[1]), "%s%d" % (nm, s), lambda q, s=s, tab=tab, lo=lo: q.tensor_tensor(B("pp", s)[:, lo:lo + 128], tab[:, csl[s]], B("msk", s)[:], A.mult))
+                    else:
+                        op("V", vgat(128), "msk%d U%s %s%d" % (s, nm[1], ct, s), "%s%d" % (nm, s), lambda q, s=s, tab=tab, lo=lo, ct=ct: q.tensor_tensor(B("pp", s)[:, lo:lo + 128], tab[:].indirect(B(ct, s)[:]), B("msk", s)[:], A.mult))
+                op("P", mm(256), "pq%d NK ones BOh" % s, "qb%d" % s, lambda q, s=s: mms(q, [
+                    (PB[s][:, 0:128], T.NK[:], T.ones[:], True, False),
+                    (PB[s][:, 0:128], T.BOh[:], B("pp", s)[:, 128:256], False, True)]), bank=bkB(s))
+                op("P", mm(16 * 64), "pw%d WR" % s, "wp%d" % s, lambda q, s=s: mms(q, [
+                    (PA[s][:, 0:8], T.WR[:, 128 * r:128 * r + 128], B("pp", s)[:, r:128:16], r == 0, r == 15) for r in range(16)]), bank=bkA(s))
+                op("S", act(128), "qb%d" % s, "tt%d" % s, lambda q, s=s: q.activation(B("tt", s)[:], PB[s][:, 0:128], F.Abs, scale=4096.0), bank=bkB(s))
+                op("V", vec(128, two=True), "tt%d zix%d" % (s, s), "cc%d" % s, lambda q, s=s: q.tensor_tensor(B("cc", s)[:], (T.zix0, T.zix1)[s][:], B("tt", s)[:], (A.add, A.subtract)[s]))
+                op("V", vec(8), "wp%d" % s, "%s%d" % (nt, s), lambda q, s=s, nt=nt: q.tensor_copy(B(nt, s)[:], PA[s][:, 0:8]), bank=bkA(s))
+                op("V", vgat(128), "%s%d cc%d %s" % (nt, s, s, eall), "ev%d" % s, lambda q, s=s, nt=nt: q.tensor_tensor(B("ev", s)[:], T.E[:].indirect(B(nt, s)[:]), B("cc", s)[:], (A.min, A.max)[s]))
+                op("V", vec(128), "ev%d" % s, "e16_%d" % s, lambda q, s=s: q.tensor_scalar(B("e16", s)[:], B("ev", s)[:], shift[s], None, A.add))
+                gather(s)
+                scans(s)
+                op("S", 90 + 128 * c_g, "%s%d BN" % (nt, s), "bg%d" % s, lambda q, s=s, nt=nt: q.activation(B("bg", s)[:], T.BN[:].indirect(B(nt, s)[:]), F.Copy))
+                op("V", vgat(128), "%s%d tt%d %s" % (nt, s, s, eall), "v1%d" % s, lambda q, s=s, nt=nt: q.tensor_tensor(B("v1", s)[:], T.E[:].indirect(B(nt, s)[:]), B("tt", s)[:], A.subtract))
+                op("S", act(128), "v1%d" % s, "dm%d%d" % (s, h), lambda q, s=s, h=h: q.activation(B("dm", s)[:, 128 * h:128 * h + 128], B("v1", s)[:], F.Sign, bias=-1535.5))
+                half(s, B("bg", s)[:], "bg%d" % s, W[:, zcol[s]], z)
+                if h == HP - 1:
+                    op("S", 90 + 128 * c_g, "%s%d Wx" % (nt, s), "xw%d" % s, lambda q, s=s, nt=nt: q.activation(B("xw", s)[:], W[:, X0:G0].indirect(B(nt, s)[:]), F.Copy))
+                    op("P", mm(256), z + " xw%d I nI" % s, "df%d" % s, lambda q, s=s: mms(q, [
+                        (PA[s][:, 0:128], T.nI[:], B("xw", s)[:], True, False),
+                        (PA[s][:, 0:128], T.I[:], W[:, zcol[s]], False, True)]), bank=bkA(s))
+                    op("S", act(128), "df%d" % s, "da%d" % s, lambda q, s=s: q.activation(B("da", s)[:], PA[s][:, 0:128], F.Abs), bank=bkA(s))
+                    op("P", mm(640), "da%d dm%d0 dm%d1 dm%d2 hs%d BO BD BH" % (s, s, s, s, s), "qq%d" % s, lambda q, s=s: mms(q, [
+                        (PB[s][:, 0:128], T.BH[:], B("hs", s)[:], True, False),
+                        (PB[s][:, 0:128], T.BD[:], B("dm", s)[:, 0:128], False, False),
+                        (PB[s][:, 0:128], T.BD[:], B("dm", s)[:, 128:256], False, False),
+                        (PB[s][:, 0:128], T.BD[:], B("dm", s)[:, 256:384], False, False),
+                        (PB[s][:, 0:128], T.BO[:], B("da", s)[:], False, True)]), bank=bkB(s))
+                    op("V", vec(128), "qq%d thr%d" % (s, t), "st%d" % s, lambda q, s=s: q.tensor_scalar(B("st", s)[:], PB[s][:, 0:128], T.thr[:, t:t + 1], None, A.is_le), bank=bkB(s))
+                    op("V", vec(128, two=True), "st%d d0%d" % (s, s), "sd%d" % s, lambda q, s=s: q.tensor_tensor(B("sd", s)[:], B("st", s)[:], B("d0", s)[:], A.mult))
+                    op("V", vec(128, two=True), "sd%d f0%d" % (s, s), "XN%d" % s, lambda q, s=s: q.tensor_tensor(T.XN[:, 128 * s:128 * s + 128], B("sd", s)[:], B("f0", s)[:], A.add))
+        if t < RO - 1:
+            op("V", vgat(128), "XN0 XN1 snd16", "XG%d" % t, lambda q: q.tensor_copy(T.XG[:, 128 * t:128 * t + 128], T.XN[:].indirect(T.snd16[:, 8 * cl:8 * cl + 8])))
+            op("R", 2000, "XG%d" % t, "sent%d" % t, lambda q: q.remote_dma(T.gl[:, 128 * t:128 * t + 128], T.XG[:, 128 * t:128 * t + 128], T.sem["ga%d" % t], T.sem["ls%d" % t], pid, rid, mask), sem=("ls%d" % t, bin(mask).count("1")))
+            op("X", 3500, "sent%d" % t, "gl%d" % t, None, sem=("ga%d" % t, bin(mask).count("1")))
+        for s in range(NS):
+            op("V", vec(128), "XN%d" % s, "Wx", lambda q, s=s: q.tensor_copy(W[:, xsl[s]], T.XN[:, 128 * s:128 * s + 128]))
+            op("V", vec(128, two=True), "hs%d st%d" % (s, s), "eu%d" % s, lambda q, s=s: q.tensor_tensor(B("eu", s)[:], B("hs", s)[:], B("st", s)[:], A.mult))
+            op("V", vec(128, two=True), "eu%d %s" % (s, ecls(s, cl)), ecls(s, cl), lambda q, s=s: q.tensor_tensor(T.E[:, csl[s]], T.E[:, csl[s]], B("eu", s)[:], A.add))
+            if t < RO - 1:
+                op("S", act(128), "st%d" % s, "rs%d junk%d" % (s, s), lambda q, s=s: q.activation(T.junk[:, 128 * s:128 * s + 128], B("st", s)[:], F.Copy, accum_out=T.rs[:, s:s + 1]))
+        if t < RO - 1:
+            op("P", mm(512), "rs0 rs1 c_os", "rp", lambda q: q.matmul(T.bk1[:, 0:2], T.c_os[:], T.rs[:], True, True), bank=1)
+            op("V", vec(2), "rp", "rsum", lambda q: q.tensor_reduce(T.rsum[:, 0:1], T.bk1[:, 0:2], AxisListType.X, A.add), bank=1)
+            op("V", vec(1), "rsum", "rint", lambda q: q.tensor_copy(T.rint[:, 0:1], T.rsum[:, 0:1]))
+            op("V", vec(1), "rint", "rand", lambda q: q.tensor_scalar(T.rand[:, 0:1], T.rint[:, 0:1], 31, None, A.bitwise_and))
+            op("V", vec(1), "rand thb", "thr%d" % (t + 1), lambda q: q.tensor_tensor(T.thr[:, t + 1:t + 2], T.thr[:, t + 1:t + 2], T.rand[:, 0:1], A.add))
+            op("V", vec(128, True), "gl%d" % t, "Wg", lambda q: q.tensor_copy(W[:, G0 + 128 * cl:G0 + 128 * cl + 128], T.gl[:, 128 * t:128 * t + 128]))
+
+    for t in range(RO):
+        one_round(t)
+    for s in range(NS):
+        dma("D", 4000, " ".join(ecls(s, c) for c in range(4)), "oe%d" % s, T.ye[:, 512 * s:512 * s + 512], T.E[:, 512 * s:512 * s + 512])
+        dma("D", 4000, "Wx", "ox%d" % s, T.yx[:, 512 * s:512 * s + 512], W[:, X0 + 512 * s:X0 + 512 * s + 512])
+    return ops
+
+
+QUEUE = {"V": "V", "S": "S", "P": "P", "G": "G", "R": "G", "D": "D", "X": "X"}
+WAKE = 80.0
+
+
+def analyse(ops):
+    lastw, readers, bank = {}, {}, {}
+    deps, order = [], []
+    for i, o in enumerate(ops):
+        d, q = set(), set()
+        for x in o["r"]:
+            if x in lastw:
+                d.add(lastw[x])
+        for x in o["w"]:
+            prev = set(readers.get(x, ()))
+            if x in lastw:
+                prev.add(lastw[x])
+            for p in prev:
+                if p != i:
+                    (q if o["eng"] == "P" and ops[p]["eng"] == "P" else d).add(p)
+        if o["bank"] is not None and o["bank"] in bank:
+            p = bank[o["bank"]]
+            (q if ops[p]["eng"] == o["eng"] else d).add(p)
+        for x in o["r"]:
+            readers.setdefault(x, set()).add(i)
+        for x in o["w"]:
+            lastw[x] = i
+            readers[x] = set()
+        if o["bank"] is not None:
+            bank[o["bank"]] = i
+        deps.append(d)
+        order.append(q)
+    return deps, order
+
+
+def schedule(ops, deps, order):
+    n = len(ops)
+    succ = [[] for _ in range(n)]
+    left = [0] * n
+    for i in range(n):
+        for p in deps[i] | order[i]:
+            succ[p].append(i)
+            left[i] += 1
+    prio = [0.0] * n
+    for i in range(n - 1, -1, -1):
+        prio[i] = ops[i]["cost"] + max([prio[j] + WAKE for j in succ[i]] + [0.0])
+    free, fin, ready = {}, [0.0] * n, [0.0] * n
+    avail = [i for i in range(n) if left[i] == 0]
+    seq = []
+    busy = {}
+    while avail:
+        best = None
+        for i in avail:
+            st = max(ready[i], free.get(QUEUE[ops[i]["eng"]], 0.0))
+            key = (st, -prio[i], i)
+            if best is None or key < best:
+                best = key
+        st, _, i = best
+        avail.remove(i)
+        seq.append(i)
+        e, c = ops[i]["eng"], ops[i]["cost"]
+        fin[i] = st + c
+        if e == "D":
+            free["D"] = st + 60
+        elif e == "R":
+            free["G"] = st + 1000
+        elif e != "X":
+            free[QUEUE[e]] = st + c
+        busy[e] = busy.get(e, 0.0) + c
+        for j in succ[i]:
+            left[j] -= 1
+            ready[j] = max(ready[j], fin[i] + (WAKE if i in deps[j] else 0.0))
+            if left[j] == 0:
+                avail.append(j)
+    return seq, fin, busy
+
+
+PLAN = {}
+
+
+def rank_program(g, core, T, topo):
+    rank = T.rank_of(core)
+    if rank is None:
+        return
+    ops = program(T, topo, core)
+    if "seq" not in PLAN:
+        deps, order = analyse(ops)
+        PLAN["deps"], PLAN["seq"] = deps, schedule(ops, deps, order)[0]
+    deps, seq = PLAN["deps"], PLAN["seq"]
+    qs = {"V": g.vector, "S": g.scalar, "P": g.tensor, "G": g, "D": g.sync}
+    count = {"V": 0, "S": 0, "P": 0, "G": 0}
+    known = {q: {} for q in qs}
+    after = {}
+    for i in seq:
+        o = ops[i]
+        if o["eng"] == "X":
+            o["done"] = o["sem"]
+            after[i] = {o["sem"][0]: o["sem"][1]}
+            continue
+        q = QUEUE[o["eng"]]
+        kn = known[q]
+        need = {}
+        for d in deps[i]:
+            nm, v = ops[d]["done"]
+            if kn.get(nm, 0) < v:
+                need[nm] = max(need.get(nm, 0), v)
+        for nm, v in need.items():
+            implied = False
+            for d in deps[i]:
+                dn, dv = ops[d]["done"]
+                if dn != nm and need.get(dn, 0) >= dv and after[d].get(nm, 0) >= v:
+                    implied = True
+            if not implied:
+                qs[q].wait_ge(T.sem[nm], v)
+        for d in deps[i]:
+            for nm, v in after[d].items():
+                if kn.get(nm, 0) < v:
+                    kn[nm] = v
+        r = o["fn"](qs[q])
+        if o["eng"] in count:
+            count[q] += 1
+            o["done"] = ("q" + q, count[q])
+            r.then_inc(T.sem["q" + q], 1)
+        else:
+            o["done"] = o["sem"]
+            if o["eng"] == "D":
+                r.then_inc(T.sem[o["sem"][0]], 16)
+        after[i] = dict(kn)
+        after[i][o["done"][0]] = o["done"][1]
+    for q in ("V", "S", "P", "G"):
+        g.wait_ge(T.sem["q" + q], count[q])
+    for o in ops:
+        if o["eng"] in ("D", "R") and known["G"].get(o["sem"][0], 0) < o["sem"][1]:
+            g.wait_ge(T.sem[o["sem"][0]], o["sem"][1])

@@ -1,22 +1,28 @@
-from concourse.mybir import dt, AluOpType, AxisListType, ActivationFunctionType
+from concourse.mybir import AluOpType, AxisListType, ActivationFunctionType
 A = AluOpType
 F = ActivationFunctionType
 
-V, H, S = 1024, 512, 1536
+S = 1536
 NS, M = 2, 128
-CH = 2
-CN = M // CH
+PIECES = [(0, 96, "S"), (96, 128, "V")]
+CH = len(PIECES)
 RO, HP = 5, 3
-X0, G0, Y0, ZB = 128, 1152, 1664, 3200
+X0, G0, Y0, WE = 128, 1152, 1664, 3200
 CMOD = 201326592.0
 CINT = 8388608.0
 HB = 1536.0
-QOFF = 196608.0 - 1024.0 * HB
+QOFF = -1024.0 * HB
+CRND = 12582912.0
+DV = (True, True)
 
 SCRATCH = {
-    "W": ("sbuf", [128, 3328], "bfloat16"),
+    "W0": ("sbuf", [128, WE], "bfloat16"),
+    "W1": ("sbuf", [128, WE], "bfloat16"),
     "enti": ("sbuf", [128, 1024], "int32"),
     "E": ("sbuf", [128, 1024], "float32"),
+    "OE": ("sbuf", [128, 1024], "float32"),
+    "CR": ("sbuf", [128, 1024], "bfloat16"),
+    "hI": ("sbuf", [128, 128], "bfloat16"),
     "usri": ("sbuf", [128, 1024], "int32"),
     "Uw": ("sbuf", [128, 1024], "int32"),
     "Uq": ("sbuf", [128, 1024], "int32"),
@@ -28,6 +34,8 @@ SCRATCH = {
     "thf": ("sbuf", [8, 5], "float32"),
     "thr": ("sbuf", [128, 8], "float32"),
     "XGi": ("sbuf", [128, 512], "bfloat16"),
+    "XG": ("sbuf", [128, 512], "bfloat16"),
+    "gl": ("sbuf", [128, 512], "bfloat16"),
     "XN": ("sbuf", [128, 256], "bfloat16"),
     "rs": ("sbuf", [128, 2], "float32"),
     "rsum": ("sbuf", [128, 8], "float32"),
@@ -48,35 +56,35 @@ SCRATCH = {
     "clist": ("sbuf", [128, 8], "uint16"),
     "c_nb": ("sbuf", [128, 8], "int32"),
     "nbase": ("sbuf", [128, 8], "bfloat16"),
-    "zix0": ("sbuf", [128, 128], "float32"),
-    "zix1": ("sbuf", [128, 128], "float32"),
+    "nt": ("sbuf", [128, 128], "bfloat16"),
     "ones": ("sbuf", [128, 128], "bfloat16"),
     "I": ("sbuf", [128, 128], "bfloat16"),
     "nI": ("sbuf", [128, 128], "bfloat16"),
     "n2I": ("sbuf", [128, 128], "bfloat16"),
     "bigI": ("sbuf", [128, 128], "bfloat16"),
     "NK": ("sbuf", [128, 128], "bfloat16"),
+    "NK4": ("sbuf", [128, 128], "bfloat16"),
     "KD": ("sbuf", [128, 128], "bfloat16"),
     "BO": ("sbuf", [128, 128], "bfloat16"),
     "BD": ("sbuf", [128, 128], "bfloat16"),
     "BH": ("sbuf", [128, 128], "bfloat16"),
     "BG": ("sbuf", [128, 8], "bfloat16"),
     "BOh": ("sbuf", [128, 128], "float16"),
-    "WR": ("sbuf", [128, 2048], "float16"),
-    "mk_mx": ("sbuf", [128, 1024], "bfloat16"),
-    "mk_mn": ("sbuf", [128, 1024], "bfloat16"),
+    "BO1": ("sbuf", [128, 128], "float16"),
+    "c_rc": ("sbuf", [128, 256], "float32"),
+    "DM": ("sbuf", [128, 256], "bfloat16"),
+    "mk_mx": ("sbuf", [128, 2048], "bfloat16"),
+    "mk_mn": ("sbuf", [128, 2048], "bfloat16"),
     "mk_ky": ("sbuf", [128, 128], "float32"),
     "ex8": ("sbuf", [8, 128], "float32"),
 }
-SCRATCH["XG"] = ("sbuf", [128, 512], "bfloat16")
-SCRATCH["gl"] = ("sbuf", [128, 512], "bfloat16")
 for _s in range(NS):
-    for _n, _w, _d in (("e16", 128, "uint16"), ("cm", 128, "bfloat16"), ("src", 2048, "bfloat16"), ("ab", 2048, "bfloat16"),
+    for _n, _w, _d in (("e16", 128, "uint16"), ("src", 2048, "bfloat16"), ("ab", 2048, "bfloat16"),
                        ("mx", 2048, "bfloat16"), ("mn", 2048, "bfloat16"), ("key", 128, "float32"), ("r1", 128, "float32"),
-                       ("hit", 128, "bfloat16"), ("hs", 128, "bfloat16"), ("pp", 256, "float16"), ("lst", 16, "uint16"),
+                       ("hit", 128, "bfloat16"), ("hs", 128, "bfloat16"), ("pp", 256, "float16"), ("wl", 256, "float16"), ("lst", 16, "uint16"),
                        ("ta", 8, "uint16"), ("tb", 8, "uint16"), ("yv", 128, "bfloat16"), ("fa", 128, "float32"),
-                       ("f0", 128, "bfloat16"), ("d0", 128, "bfloat16"), ("r16", 128, "bfloat16"), ("msk", 128, "bfloat16"),
-                       ("tt", 128, "float32"), ("cc", 128, "float32"), ("ev", 128, "float32"), ("v1", 128, "float32"),
+                       ("r16", 128, "bfloat16"), ("msk", 128, "bfloat16"), ("dv", 512, "bfloat16"),
+                       ("tt", 128, "float32"), ("rr", 128, "bfloat16"), ("cg", 128, "bfloat16"),
                        ("dm", 384, "bfloat16"), ("bg", 128, "bfloat16"),
                        ("xw", 128, "bfloat16"), ("da", 128, "bfloat16"), ("st", 128, "bfloat16"), ("sd", 128, "bfloat16"),
                        ("eu", 128, "bfloat16")):
@@ -87,33 +95,38 @@ for _b in range(8):
 SEMAPHORES = ["qV", "qS", "qP", "qG", "gini", "lini"] + ["ga%d" % t for t in range(4)] + ["ls%d" % t for t in range(4)] + ["d%d" % i for i in range(24)]
 
 CY = 0.83
+EST = {"fv": 30.0, "fs": 70.0, "fp": 25.0, "c": 1.45, "sc": 3.5, "wake": 70.0, "bias": 0.0, "remote": 3500.0, "ld": 1.0, "look": 60.0}
 
 
 def program(T, topo, core):
     ops = []
-    c_g = 1.5 * CY
+    c_g = EST["c"] * CY
+    ctx = [0]
 
-    def op(eng, cost, reads, writes, fn, bank=None, sem=None):
-        ops.append(dict(eng=eng, cost=cost, r=reads.split(), w=writes.split(), fn=fn, bank=bank, sem=sem))
+    def op(eng, cost, reads, writes, fn, bank=None, sem=None, after=""):
+        ops.append(dict(eng=eng, cost=cost, r=reads.split(), w=writes.split(), fn=fn, bank=bank, sem=sem, s=ctx[0], after=after.split()))
 
     def vec(n, half=False, two=False):
-        return 60 + max(64, n * (0.5 if half else 2 if two else 1)) * CY
+        return EST["fv"] + max(64, n * (0.5 if half else 2 if two else 1)) * CY
 
     def vgat(n):
-        return 60 + n * c_g
+        return 50 + n * c_g
 
     def act(n):
-        return 90 + n * CY
+        return EST["fs"] + n * CY
+
+    def sgat(n):
+        return 65 + n * c_g
 
     def mm(cy):
-        return 60 + cy * CY
+        return EST["fp"] + cy * CY
 
     B = lambda n, s: T["%s_%d" % (n, s)]
-    rank = T.rank_of(core)
-    dst = T.cores[(rank - 1) % 4]
+    dst = T.cores[(T.rank_of(core) - 1) % 4]
     rid, pid = topo.addr(dst)[0], topo.addr(dst)[1]
-    mask = topo.mask(core, dst)
-    W = T.W
+    mask, neng = topo.mask(core, dst), len(topo.engines(core, dst))
+    W = (T.W0, T.W1)
+    ld = EST["ld"]
 
     dn = [0]
 
@@ -122,30 +135,33 @@ def program(T, topo, core):
         dn[0] += 1
         op(eng, cost, reads, writes, (lambda q, out=out, in_=in_: q.dma_start(out, in_)), sem=(name, 16))
 
-    dma("D", 3000, "", "sndi", T.sndi[:], T.snd[:])
-    dma("D", 3500, "", "Wx", W[:, X0:G0], T.xa[:])
-    dma("D", 5000, "", "enti", T.enti[:], T.ent[:])
-    dma("D", 6500, "", "Wy", W[:, Y0:ZB], T.yc[:])
-    dma("D", 8000, "", "BN", T.BN[:], T.bn[:])
-    dma("D", 9500, "", "usri", T.usri[:], T.usr[:])
-    dma("D", 10000, "", "thi", T.thi[:], T.th[:])
+    dma("D", 2500 * ld, "", "sndi", T.sndi[:], T.snd[:])
+    dma("D", 3000 * ld, "", "Wx0", W[0][:, X0:G0], T.xa[:])
+    dma("DS", 5500 * ld, "", "enti", T.enti[:], T.ent[:])
+    dma("D", 7000 * ld, "", "Wy0", W[0][:, Y0:WE], T.yc[:])
+    dma("DS", 8000 * ld, "", "Wx1", W[1][:, X0:G0], T.xa[:])
+    dma("D", 9000 * ld, "", "Wy1", W[1][:, Y0:WE], T.yc[:])
+    dma("DS", 10000 * ld, "", "BN", T.BN[:], T.bn[:])
+    dma("D", 12000 * ld, "", "usri", T.usri[:], T.usr[:])
+    dma("DS", 12000 * ld, "", "thi", T.thi[:], T.th[:])
 
     for c in range(4):
-        op("V", vec(8), "sndi", "gi16", lambda q, c=c: q.tensor_scalar(T.gi16[:, 8 * c:8 * c + 8], T.sndi[:, 8 * c:8 * c + 8], 4, c, A.mult, A.add))
-    op("V", vgat(512), "gi16 Wx", "XGi", lambda q: q.tensor_copy(T.XGi[:], W[:, X0:G0].indirect(T.gi16[:])))
-    op("R", 2000, "XGi", "sent", lambda q: q.remote_dma(T.W[:, G0:Y0], T.XGi[:], T.sem["gini"], T.sem["lini"], pid, rid, mask), sem=("lini", bin(mask).count("1")))
-    op("X", 5000, "sent", "Wg", None, sem=("gini", bin(mask).count("1")))
+        op("V", vec(8), "sndi", "gi16%d" % c, lambda q, c=c: q.tensor_scalar(T.gi16[:, 8 * c:8 * c + 8], T.sndi[:, 8 * c:8 * c + 8], 4, c, A.mult, A.add))
+    op("V", vgat(512), "gi160 gi161 gi162 gi163 Wx0", "XGi", lambda q: q.tensor_copy(T.XGi[:], W[0][:, X0:G0].indirect(T.gi16[:])))
+    op("R", 2000, "XGi", "sent", lambda q: q.remote_dma(W[0][:, G0:Y0], T.XGi[:], T.sem["gini"], T.sem["lini"], pid, rid, mask), sem=("lini", neng))
+    op("X", 5000, "sent", "Wg0", None, sem=("gini", neng))
+    op("V", vec(512, True), "Wg0", "Wg1", lambda q: q.tensor_copy(W[1][:, G0:Y0], W[0][:, G0:Y0]))
     op("V", vec(32), "sndi", "snd16", lambda q: q.tensor_copy(T.snd16[:], T.sndi[:]))
 
     op("V", vec(128), "", "c_one", lambda q: q.memset(T.c_one[:], 1.0))
     op("V", vec(128), "", "ones", lambda q: q.memset(T.ones[:], 1.0))
     op("V", vec(128), "", "c_os", lambda q: q.memset(T.c_os[:], 0.0625))
-    op("V", vec(128), "", "za0", lambda q: q.memset(W[:, 0:X0], 0.0))
-    op("V", vec(128), "", "za1", lambda q: q.memset(W[:, ZB:ZB + 128], 0.0))
+    op("V", vec(128), "", "za0", lambda q: q.memset(W[0][:, 0:X0], 0.0))
+    op("V", vec(128), "", "za1", lambda q: q.memset(W[1][:, 0:X0], 0.0))
     op("V", vec(1024, True), "", "mk_mx", lambda q: q.memset(T.mk_mx[:], 255.0))
-    op("V", vec(64), "", "mk_mx", lambda q: q.memset(T.mk_mx[:, 0:1024:16], 0.0))
+    op("V", vec(64), "", "mk_mx", lambda q: q.memset(T.mk_mx[:, 0:2048:16], 0.0))
     op("V", vec(1024, True), "", "mk_mn", lambda q: q.memset(T.mk_mn[:], 0.0))
-    op("V", vec(64), "", "mk_mn", lambda q: q.memset(T.mk_mn[:, 0:1024:16], 255.0))
+    op("V", vec(64), "", "mk_mn", lambda q: q.memset(T.mk_mn[:, 0:2048:16], 255.0))
     op("V", vec(128), "", "mk_ky", lambda q: q.memset(T.mk_ky[:], 0.0))
     op("V", vec(64), "", "mk_ky", lambda q: q.memset(T.mk_ky[:, 0:128:16], 131071.0))
     op("G", 400, "c_one", "c_if", lambda q: q.affine_select(T.c_if[:], T.c_one[:], [[-1, 128]], A.is_equal, 0.0, 0, 1))
@@ -154,9 +170,8 @@ def program(T, topo, core):
     op("G", 200, "", "c_pi", lambda q: q.iota(T.c_pi[:], [[0, 1]], 0, 1))
     op("G", 200, "", "c_cl", lambda q: q.iota(T.c_cl[:], [[16, 8]], 15, 0))
     op("G", 200, "", "c_nb", lambda q: q.iota(T.c_nb[:], [[256, 8]], 0, 0))
-    op("G", 400, "", "zix0", lambda q: q.iota(T.zix0[:], [[1, 128]], -128, 0, allow_small_or_imprecise_dtypes=True))
-    op("G", 400, "", "zix1", lambda q: q.iota(T.zix1[:], [[1, 128]], 3072, 0, allow_small_or_imprecise_dtypes=True))
-    op("G", 400, "c_one", "ex8t", lambda q: q.affine_select(T.ex8[:], T.c_one[0:8, :], [[-1, 8], [0, 16]], A.is_equal, 0.0, 0, 1))
+    op("G", 400, "", "nt", lambda q: q.iota(T.nt[:], [[1, 128]], 0, 0, allow_small_or_imprecise_dtypes=True))
+    op("G", 400, "c_one", "ex8", lambda q: q.affine_select(T.ex8[:], T.c_one[0:8, :], [[-1, 8], [0, 16]], A.is_equal, 0.0, 0, 1))
     op("V", vec(1), "c_pi", "c_ki", lambda q: q.tensor_scalar(T.c_ki[:], T.c_pi[:], 15, None, A.bitwise_and))
     op("V", vec(1), "c_ki", "kcol", lambda q: q.tensor_copy(T.kcol[:], T.c_ki[:]))
     op("V", vec(1), "kcol", "nkcol", lambda q: q.tensor_scalar(T.nkcol[:], T.kcol[:], -1.0, None, A.mult))
@@ -166,20 +181,21 @@ def program(T, topo, core):
     op("V", vec(128), "c_if", "I", lambda q: q.tensor_copy(T.I[:], T.c_if[:]))
     op("V", vec(128), "c_if", "nI", lambda q: q.tensor_scalar(T.nI[:], T.c_if[:], -1.0, None, A.mult))
     op("V", vec(128), "c_if", "n2I", lambda q: q.tensor_scalar(T.n2I[:], T.c_if[:], -2.0, None, A.mult))
+    op("V", vec(128), "c_if", "hI", lambda q: q.tensor_scalar(T.hI[:], T.c_if[:], -0.5, None, A.mult))
     op("V", vec(128), "c_if", "bigI", lambda q: q.tensor_scalar(T.bigI[:], T.c_if[:], 131072.0, None, A.mult))
     op("V", vec(128), "c_if nkcol", "NK", lambda q: q.tensor_scalar(T.NK[:], T.c_if[:], T.nkcol[:], None, A.mult))
+    op("V", vec(128), "c_if nkcol", "NK4", lambda q: q.tensor_scalar(T.NK4[:], T.c_if[:], T.nkcol[:], 4096.0, A.mult, A.mult))
     op("V", vec(128), "c_if kcol", "KD", lambda q: q.tensor_scalar(T.KD[:], T.c_if[:], T.kcol[:], None, A.mult))
     op("V", vec(128), "c_bof", "BO", lambda q: q.tensor_copy(T.BO[:], T.c_bof[:]))
-    op("V", vec(128), "c_bof", "BD", lambda q: q.tensor_scalar(T.BD[:], T.c_bof[:], -4096.0, None, A.mult))
+    op("V", vec(128), "c_bof", "BD", lambda q: q.tensor_scalar(T.BD[:], T.c_bof[:], -8192.0, None, A.mult))
     op("V", vec(128), "c_bof", "BH", lambda q: q.tensor_scalar(T.BH[:], T.c_bof[:], -1024.0, None, A.mult))
     op("V", vec(8), "c_bof", "BG", lambda q: q.tensor_scalar(T.BG[:], T.c_bof[:, 0:128:16], 16.0, None, A.mult))
-    op("V", vec(128), "c_bof", "BOh", lambda q: q.tensor_copy(T.BOh[:], T.c_bof[:]))
-    for h in range(2):
-        op("V", vec(1024, True), "mk_mn", "WR", lambda q, h=h: q.tensor_scalar(T.WR[:, 1024 * h:1024 * h + 1024], T.mk_mn[:], 0.0, None, A.mult))
-    for r in range(16):
-        op("V", vec(8), "c_bof", "WR", lambda q, r=r: q.tensor_copy(T.WR[:, 128 * r + r:128 * r + 128:16], T.c_bof[:, 0:128:16]))
+    op("V", vec(128), "c_bof", "BOh", lambda q: q.tensor_scalar(T.BOh[:], T.c_bof[:], 4096.0, None, A.mult))
+    op("V", vec(128), "c_bof", "BO1", lambda q: q.tensor_copy(T.BO1[:], T.c_bof[:]))
+    op("G", 600, "", "c_rc", lambda q: q.iota(T.c_rc[:], [[0, 16], [1, 16]], 0, 0, allow_small_or_imprecise_dtypes=True))
+    op("V", vec(256), "c_rc kcol", "DM", lambda q: q.tensor_scalar(T.DM[:], T.c_rc[:], T.kcol[:], None, A.is_equal))
     op("V", vec(5), "thi", "thf", lambda q: q.tensor_copy(T.thf[:], T.thi[:]))
-    op("P", mm(512), "thf ex8t", "ps_th", lambda q: q.matmul(T.bk0[:, 0:5], T.ex8[:], T.thf[:], True, True), bank=0)
+    op("P", mm(512), "thf ex8", "ps_th", lambda q: q.matmul(T.bk0[:, 0:5], T.ex8[:], T.thf[:], True, True), bank=0)
     op("V", vec(5), "ps_th", "thb thr0", lambda q: q.tensor_scalar(T.thr[:, 0:5], T.bk0[:, 0:5], QOFF, None, A.add), bank=0)
 
     ecls = lambda s, cl: "E%d%d" % (s, cl)
@@ -187,7 +203,9 @@ def program(T, topo, core):
     for cl in range(4):
         for s in range(NS):
             sl = slice(512 * s + cl, 512 * s + 512, 4)
-            op("V", vec(128), "enti", ecls(s, cl), lambda q, sl=sl: q.tensor_copy(T.E[:, sl], T.enti[:, sl]))
+            op("V", vec(128), "enti", ecls(s, cl), lambda q, sl=sl: q.tensor_scalar(T.E[:, sl], T.enti[:, sl], X0, None, A.add))
+            op("V", vec(128), "enti", "C" + ecls(s, cl), lambda q, sl=sl: q.tensor_scalar(T.CR[:, sl], T.enti[:, sl], S, None, A.is_ge))
+    call = " ".join("C" + x for x in eall.split())
     op("V", vec(1024), "usri", "Uq", lambda q: q.tensor_scalar(T.Uq[:], T.usri[:], 15, None, A.bitwise_and))
     op("V", vec(1024), "usri", "Uw", lambda q: q.tensor_scalar(T.Uw[:], T.usri[:], 4, None, A.arith_shift_right))
 
@@ -197,152 +215,194 @@ def program(T, topo, core):
             r = q.matmul(*a)
         return r
 
-    zcol = (slice(0, 128), slice(ZB, ZB + 128))
-    wins = (slice(0, ZB), slice(X0, ZB + 128))
-    shift = (float(X0), 0.0)
-
     def bkA(s): return 2 * s
     def bkB(s): return 2 * s + 1
     PA = (T.bk0, T.bk2)
     PB = (T.bk1, T.bk3)
-    PJ = (T.bk4, T.bk5, T.bk6, T.bk7)
+    PJ = (T.bk4, T.bk5, T.bk6)
+    F0 = (T.bk7[:, 0:128], T.bk7[:, 128:256])
+    VB = (T.bk7[:, 256:384], T.bk7[:, 384:512])
+    zcol = slice(0, X0)
 
     def gather(s):
-        z = "za%d" % s
-        for c in range(CH):
-            op("S", 90 + 16 * CN * c_g, "e16_%d Wx Wg Wy %s" % (s, z), "src%d%d" % (s, c),
-               lambda q, s=s, c=c: q.activation(B("src", s)[:, 16 * CN * c:16 * CN * (c + 1)], W[:, wins[s]].indirect(B("e16", s)[:, CN * c:CN * (c + 1)]), F.Copy))
+        for c, (lo, hi, who) in enumerate(PIECES):
+            n = 16 * (hi - lo)
+            rd, wr = "e16_%d Wx%d Wg%d Wy%d za%d" % (s, s, s, s, s), "src%d%d" % (s, c)
+            out, in_ = B("src", s)[:, 16 * lo:16 * hi], W[s][:, 0:WE].indirect(B("e16", s)[:, lo:hi])
+            if who == "S":
+                op("S", sgat(n), rd, wr, lambda q, out=out, in_=in_: q.activation(out, in_, F.Copy))
+            else:
+                op("V", vgat(n), rd, wr, lambda q, out=out, in_=in_: q.tensor_copy(out, in_))
 
     def scans(s):
-        for c in range(CH):
-            sl = slice(16 * CN * c, 16 * CN * (c + 1))
-            op("V", vec(16 * CN, True), "src%d%d mk_mx" % (s, c), "mx%d%d" % (s, c),
-               lambda q, s=s, sl=sl: q.tensor_tensor_scan(B("mx", s)[:, sl], T.mk_mx[:, 0:16 * CN], B("src", s)[:, sl], 0.0, A.min, A.max))
-            op("V", vec(16 * CN, True), "src%d%d mk_mn" % (s, c), "mn%d%d" % (s, c),
-               lambda q, s=s, sl=sl: q.tensor_tensor_scan(B("mn", s)[:, sl], T.mk_mn[:, 0:16 * CN], B("src", s)[:, sl], 255.0, A.max, A.min))
+        for c, (lo, hi, who) in enumerate(PIECES):
+            n, sl = 16 * (hi - lo), slice(16 * lo, 16 * hi)
+            op("V", vec(n, True), "src%d%d mk_mx" % (s, c), "mx%d%d" % (s, c),
+               lambda q, s=s, sl=sl, n=n: q.tensor_tensor_scan(B("mx", s)[:, sl], T.mk_mx[:, 0:n], B("src", s)[:, sl], 0.0, A.min, A.max))
+            op("V", vec(n, True), "src%d%d mk_mn" % (s, c), "mn%d%d" % (s, c),
+               lambda q, s=s, sl=sl, n=n: q.tensor_tensor_scan(B("mn", s)[:, sl], T.mk_mn[:, 0:n], B("src", s)[:, sl], 255.0, A.max, A.min))
 
-    def half(s, bsrc, btok, out, otok):
-        rd = " ".join("mx%d%d mn%d%d" % (s, c, s, c) for c in range(CH))
-        op("P", mm(384), rd + " I n2I " + btok, "h%d" % s, lambda q, s=s: mms(q, [
-            (PA[s][:, 0:128], T.n2I[:], bsrc, True, False),
-            (PA[s][:, 0:128], T.I[:], B("mx", s)[:, 15:2048:16], False, False),
-            (PA[s][:, 0:128], T.I[:], B("mn", s)[:, 15:2048:16], False, True)]), bank=bkA(s))
-        op("S", act(128), "h%d" % s, "fa%d" % s, lambda q, s=s: q.activation(B("fa", s)[:], PA[s][:, 0:128], F.Abs, bias=-0.25, scale=0.5), bank=bkA(s))
-        op("V", vec(128), "fa%d" % s, otok, lambda q, s=s: q.tensor_scalar(out, B("fa", s)[:], CINT, CINT, A.add, A.subtract))
+    def half(s, bsrc, btok, out, otok, bank=None):
+        op("P", mm(256), "n2I hI ones " + btok, "h%d" % s, lambda q, s=s: mms(q, [
+            (PA[s][:, 0:128], T.hI[:], T.ones[:], True, False),
+            (PA[s][:, 0:128], T.n2I[:], bsrc, False, False)]), bank=bkA(s))
+        op("P", mm(128), "I " + " ".join("mx%d%d" % (s, c) for c in range(CH)), "h%d" % s, lambda q, s=s: q.matmul(PA[s][:, 0:128], T.I[:], B("mx", s)[:, 15:2048:16], False, False), bank=bkA(s))
+        op("P", mm(128), "I " + " ".join("mn%d%d" % (s, c) for c in range(CH)), "h%d" % s, lambda q, s=s: q.matmul(PA[s][:, 0:128], T.I[:], B("mn", s)[:, 15:2048:16], False, True), bank=bkA(s))
+        if bank is not None:
+            op("S", act(128), "h%d" % s, "fa%d" % s, lambda q, s=s: q.activation(B("fa", s)[:], PA[s][:, 0:128], F.Abs, scale=0.5), bank=bkA(s))
+            op("V", vec(128), "fa%d" % s, otok, lambda q, s=s: q.tensor_scalar(out, B("fa", s)[:], CINT, CINT, A.add, A.subtract), bank=bank)
+        else:
+            op("S", act(128), "h%d" % s, "fa%d" % s, lambda q, s=s: q.activation(B("fa", s)[:], PA[s][:, 0:128], F.Identity, bias=CRND, scale=0.5), bank=bkA(s))
+            op("S", act(128), "fa%d" % s, otok, lambda q, s=s: q.activation(out, B("fa", s)[:], F.Abs, bias=-CRND))
+
+    def fold(s, k):
+        rd = ("pw%d" % s, "pw%d pq%d" % (s, s))[k - 1]
+        op("P", mm(128 * k), rd + " BO1", "wi%d" % s, lambda q, s=s: mms(q, [
+            (PA[s][:, 128 + 128 * j:256 + 128 * j], B("pp", s)[:, 128 * j:128 * j + 128], T.BO1[:], True, True) for j in range(k)]), bank=bkA(s), after="qb%d" % s if k == 1 else "")
+        op("V", vec(128 * k), "wi%d DM" % s, "wl%d" % s, lambda q, s=s: q.tensor_tensor(B("wl", s)[:, 0:128 * k], PA[s][:, 128:128 + 128 * k], T.DM[:, 0:128 * k], A.mult), bank=bkA(s))
+        op("P", mm(64 * (2 * k - 1)), "wl%d BO1 I nbase" % s, "wp%d" % s, lambda q, s=s: mms(q, [
+            (PA[s][:, 384:392], B("wl", s)[:, 0:128], T.BO1[:, 0:128:16], True, True)] + ([
+                (PA[s][:, 392:400], B("wl", s)[:, 128:256], T.BO1[:, 0:128:16], True, False),
+                (PA[s][:, 392:400], T.I[:], T.nbase[:], False, True)] if k == 2 else [])), bank=bkA(s))
 
     def one_round(t):
         cl = t % 4
+        last = t == RO - 1
         csl = [slice(512 * s + cl, 512 * s + 512, 4) for s in range(NS)]
         xsl = [slice(X0 + 512 * s + cl, X0 + 512 * s + 512, 4) for s in range(NS)]
         for s in range(NS):
+            ctx[0] = s
             ec = ecls(s, cl)
-            op("V", vec(128), ec, "e16_%d" % s, lambda q, s=s: q.tensor_scalar(B("e16", s)[:], T.E[:, csl[s]], shift[s], None, A.add))
-            op("V", vec(128), ec, "cm%d" % s, lambda q, s=s: q.tensor_scalar(B("cm", s)[:], T.E[:, csl[s]], float(S), None, A.is_ge))
+            op("V", vec(128), ec, "e16_%d" % s, lambda q, s=s: q.tensor_copy(B("e16", s)[:], T.E[:, csl[s]]))
             gather(s)
             sr = " ".join("src%d%d" % (s, c) for c in range(CH))
-            op("P", mm(256), "ones KD cm%d bigI" % s, "ky%d" % s, lambda q, s=s: mms(q, [
+            op("P", mm(256), "ones KD C%s bigI" % ec, "ky%d" % s, lambda q, s=s: mms(q, [
                 (PB[s][:, 0:128], T.ones[:], T.KD[:], True, False),
-                (PB[s][:, 0:128], B("cm", s)[:], T.bigI[:], False, False)]), bank=bkB(s))
-            for b in range(4):
-                op("P", mm(1024), sr + " I nI Wx", "j%d" % b, lambda q, s=s, b=b: mms(q, [
-                    a for k in range(4) for a in (
-                        (PJ[b][:, 128 * k:128 * k + 128], T.I[:], B("src", s)[:, 4 * b + k:2048:16], True, False),
-                        (PJ[b][:, 128 * k:128 * k + 128], T.nI[:], W[:, xsl[s]], False, True))]), bank=4 + b)
-                op("S", act(512), "j%d" % b, "ab%d%d" % (s, b), lambda q, s=s, b=b: q.activation(B("ab", s)[:, 512 * b:512 * b + 512], PJ[b][:], F.Abs), bank=4 + b)
+                (PB[s][:, 0:128], T.CR[:, csl[s]], T.bigI[:], False, False)]), bank=bkB(s))
+            for b in (3, 0, 1, 2):
+                out = slice(512 * b, 512 * b + 512)
+                if b == 3 and DV[s]:
+                    for k in range(4):
+                        op("V", vec(128, two=True), sr + " Wx%d" % s, "dv%d%d" % (s, k), lambda q, s=s, k=k: q.tensor_tensor(
+                            B("dv", s)[:, 128 * k:128 * k + 128], B("src", s)[:, 12 + k:2048:16], W[s][:, xsl[s]], A.subtract))
+                    op("S", act(512), " ".join("dv%d%d" % (s, k) for k in range(4)), "ab%d%d" % (s, b), lambda q, s=s, out=out: q.activation(B("ab", s)[:, out], B("dv", s)[:], F.Abs))
+                else:
+                    j = b % 3
+                    op("P", mm(1024), sr + " I nI Wx%d" % s, "j%d" % j, lambda q, s=s, b=b, j=j: mms(q, [
+                        a for k in range(4) for a in (
+                            (PJ[j][:, 128 * k:128 * k + 128], T.I[:], B("src", s)[:, 4 * b + k:2048:16], True, False),
+                            (PJ[j][:, 128 * k:128 * k + 128], T.nI[:], W[s][:, xsl[s]], False, True))]), bank=4 + j)
+                    op("S", act(512), "j%d" % j, "ab%d%d" % (s, b), lambda q, s=s, out=out, j=j: q.activation(B("ab", s)[:, out], PJ[j][:], F.Abs), bank=4 + j)
+            for b in (0, 1, 3, 2):
                 op("P", mm(256), "ab%d%d BG" % (s, b), "ky%d" % s, lambda q, s=s, b=b: mms(q, [
-                    (PB[s][:, k:128:16], B("ab", s)[:, 128 * k:128 * k + 128], T.BG[:], False, k == 15) for k in range(4 * b, 4 * b + 4)]), bank=bkB(s))
+                    (PB[s][:, k:128:16], B("ab", s)[:, 128 * k:128 * k + 128], T.BG[:], False, k == 11) for k in range(4 * b, 4 * b + 4)]), bank=bkB(s))
             scans(s)
-            half(s, T.BN[:, csl[s]], "BN", B("f0", s)[:], "f0%d" % s)
+            half(s, T.BN[:, csl[s]], "BN", F0[s], "f0%d" % s, 7)
             op("S", act(128), "ky%d" % s, "key%d" % s, lambda q, s=s: q.activation(B("key", s)[:], PB[s][:, 0:128], F.Copy), bank=bkB(s))
             op("V", vec(128), "key%d mk_ky" % s, "r1%d" % s, lambda q, s=s: q.tensor_tensor_scan(B("r1", s)[:], T.mk_ky[:], B("key", s)[:], 131071.0, A.max, A.min))
             op("V", vgat(128), "r1%d key%d clist" % (s, s), "hit%d" % s, lambda q, s=s: q.tensor_tensor(B("hit", s)[:], B("r1", s)[:].indirect(T.clist[:]), B("key", s)[:], A.is_equal))
-            op("P", mm(128), "hit%d I" % s, "ht%d" % s, lambda q, s=s: q.matmul(PA[s][:, 0:128], B("hit", s)[:], T.I[:], True, True), bank=bkA(s))
-            op("V", vec(128), "ht%d %s" % (s, ec), "pw%d" % s, lambda q, s=s: q.tensor_tensor(B("pp", s)[:, 0:128], PA[s][:, 0:128], T.E[:, csl[s]], A.mult), bank=bkA(s))
-            op("V", vec(128), "ht%d kcol" % s, "pq%d" % s, lambda q, s=s: q.tensor_scalar(B("pp", s)[:, 128:256], PA[s][:, 0:128], T.kcol[:], None, A.mult), bank=bkA(s))
-            op("S", act(128), "ht%d" % s, "hs%d" % s, lambda q, s=s: q.activation(B("hs", s)[:], PA[s][:, 0:128], F.Copy, scale=HB), bank=bkA(s))
-            op("P", mm(17 * 64), "pw%d pq%d WR I nbase" % (s, s), "wp%d" % s, lambda q, s=s: mms(q, [
-                (PB[s][:, 0:16], T.WR[:, 128 * r:128 * r + 128], B("pp", s)[:, r:256:16], r == 0, False) for r in range(16)] + [
-                (PB[s][:, 8:16], T.I[:], T.nbase[:], False, True)]), bank=bkB(s))
-            op("V", vec(16), "wp%d" % s, "lst%d" % s, lambda q, s=s: q.tensor_copy(B("lst", s)[:], PB[s][:, 0:16]), bank=bkB(s))
-            op("V", vgat(128), "lst%d Wy" % s, "yv%d" % s, lambda q, s=s: q.tensor_copy(B("yv", s)[:], W[:, Y0:ZB].indirect(B("lst", s)[:, 0:8])))
-            allsrc = " ".join("src%d%d" % (s, c) for c in range(CH))
-            op("V", 60 + 128 * 3.5 * CY, "lst%d yv%d" % (s, s), allsrc, lambda q, s=s: q.tensor_copy(B("src", s)[:].indirect(B("lst", s)[:, 8:16]), B("yv", s)[:]))
+            op("P", mm(128), "hit%d I" % s, "ht%d" % s, lambda q, s=s: q.matmul(PB[s][:, 256:384], B("hit", s)[:], T.I[:], True, True), bank=bkB(s))
+            op("V", vec(128), "ht%d %s" % (s, ec), "pw%d" % s, lambda q, s=s: q.tensor_tensor(B("pp", s)[:, 0:128], PB[s][:, 256:384], T.E[:, csl[s]], A.mult), bank=bkB(s))
+            op("V", vec(128), "ht%d kcol" % s, "pq%d" % s, lambda q, s=s: q.tensor_scalar(B("pp", s)[:, 128:256], PB[s][:, 256:384], T.kcol[:], None, A.mult), bank=bkB(s))
+            fold(s, 2)
+            op("S", act(128), "ht%d" % s, "hs%d" % s, lambda q, s=s: q.activation(B("hs", s)[:], PB[s][:, 256:384], F.Copy, scale=HB), bank=bkB(s))
+            op("V", vec(16), "wp%d" % s, "lst%d" % s, lambda q, s=s: q.tensor_copy(B("lst", s)[:], PA[s][:, 384:400]), bank=bkA(s))
+            op("S", sgat(128), "lst%d Wy%d Wg%d" % (s, s, s), "yv%d" % s, lambda q, s=s: q.activation(B("yv", s)[:], W[s][:, Y0 - X0:WE].indirect(B("lst", s)[:, 0:8]), F.Copy))
+            op("V", 50 + 128 * EST["sc"] * CY, "lst%d yv%d" % (s, s), sr, lambda q, s=s: q.tensor_copy(B("src", s)[:].indirect(B("lst", s)[:, 8:16]), B("yv", s)[:]))
             scans(s)
-            half(s, T.BN[:, csl[s]], "BN", W[:, zcol[s]], "za%d" % s)
-            op("V", vec(128, two=True), "za%d f0%d" % (s, s), "d0%d" % s, lambda q, s=s: q.tensor_tensor(B("d0", s)[:], W[:, zcol[s]], B("f0", s)[:], A.subtract))
+            half(s, T.BN[:, csl[s]], "BN", W[s][:, zcol], "za%d" % s)
         for h in range(HP):
             for s in range(NS):
+                ctx[0] = s
                 z = "za%d" % s
                 nt, ct = ("ta", "tb")[h % 2], ("tb", "ta")[h % 2]
-                op("P", mm(256), z + " NK ones BO", "s%d" % s, lambda q, s=s: mms(q, [
-                    (PA[s][:, 0:128], T.NK[:], T.ones[:], True, False),
-                    (PA[s][:, 0:128], T.BO[:], W[:, zcol[s]], False, True)]), bank=bkA(s))
+                op("P", mm(128), "NK ones", "s%d" % s, lambda q, s=s: q.matmul(PA[s][:, 0:128], T.NK[:], T.ones[:], True, False), bank=bkA(s))
+                op("P", mm(128), z + " BO", "s%d" % s, lambda q, s=s: q.matmul(PA[s][:, 0:128], T.BO[:], W[s][:, zcol], False, True), bank=bkA(s))
                 op("V", vec(128), "s%d" % s, "r16%d" % s, lambda q, s=s: q.tensor_scalar(B("r16", s)[:], PA[s][:, 0:128], CMOD, CMOD, A.add, A.subtract), bank=bkA(s))
-                op("V", vec(128), "s%d r16%d" % (s, s), "msk%d" % s, lambda q, s=s: q.tensor_tensor(B("msk", s)[:], PA[s][:, 0:128], B("r16", s)[:], A.is_equal), bank=bkA(s))
-                for nm, tab, lo in (("pq", T.Uq, 128), ("pw", T.Uw, 0)):
+                if h == 0:
+                    op("V", vec(128), "s%d r16%d" % (s, s), "vb%d" % s, lambda q, s=s: q.tensor_tensor(VB[s], PA[s][:, 0:128], B("r16", s)[:], A.is_equal), bank=bkA(s))
+                else:
+                    op("V", vec(128), "s%d r16%d" % (s, s), "msk%d" % s, lambda q, s=s: q.tensor_tensor(B("msk", s)[:], PA[s][:, 0:128], B("r16", s)[:], A.is_equal), bank=bkA(s))
+                for nm, tab, lo, aft in (("pq", T.Uq, 128, ""), ("pw", T.Uw, 0, "pq%d" % s)):
                     if h == 0:
-                        op("V", vec(128, two=True), "msk%d U%s" % (s, nm[1]), "%s%d" % (nm, s), lambda q, s=s, tab=tab, lo=lo: q.tensor_tensor(B("pp", s)[:, lo:lo + 128], tab[:, csl[s]], B("msk", s)[:], A.mult))
+                        op("V", vec(128), "vb%d U%s" % (s, nm[1]), "%s%d" % (nm, s), lambda q, s=s, tab=tab, lo=lo: q.tensor_tensor(B("pp", s)[:, lo:lo + 128], tab[:, csl[s]], VB[s], A.mult), bank=7, after=aft)
                     else:
-                        op("V", vgat(128), "msk%d U%s %s%d" % (s, nm[1], ct, s), "%s%d" % (nm, s), lambda q, s=s, tab=tab, lo=lo, ct=ct: q.tensor_tensor(B("pp", s)[:, lo:lo + 128], tab[:].indirect(B(ct, s)[:]), B("msk", s)[:], A.mult))
-                op("P", mm(256), "pq%d NK ones BOh" % s, "qb%d" % s, lambda q, s=s: mms(q, [
-                    (PB[s][:, 0:128], T.NK[:], T.ones[:], True, False),
-                    (PB[s][:, 0:128], T.BOh[:], B("pp", s)[:, 128:256], False, True)]), bank=bkB(s))
-                op("P", mm(16 * 64), "pw%d WR" % s, "wp%d" % s, lambda q, s=s: mms(q, [
-                    (PA[s][:, 0:8], T.WR[:, 128 * r:128 * r + 128], B("pp", s)[:, r:128:16], r == 0, r == 15) for r in range(16)]), bank=bkA(s))
-                op("S", act(128), "qb%d" % s, "tt%d" % s, lambda q, s=s: q.activation(B("tt", s)[:], PB[s][:, 0:128], F.Abs, scale=4096.0), bank=bkB(s))
-                op("V", vec(128, two=True), "tt%d zix%d" % (s, s), "cc%d" % s, lambda q, s=s: q.tensor_tensor(B("cc", s)[:], (T.zix0, T.zix1)[s][:], B("tt", s)[:], (A.add, A.subtract)[s]))
-                op("V", vec(8), "wp%d" % s, "%s%d" % (nt, s), lambda q, s=s, nt=nt: q.tensor_copy(B(nt, s)[:], PA[s][:, 0:8]), bank=bkA(s))
-                op("V", vgat(128), "%s%d cc%d %s" % (nt, s, s, eall), "ev%d" % s, lambda q, s=s, nt=nt: q.tensor_tensor(B("ev", s)[:], T.E[:].indirect(B(nt, s)[:]), B("cc", s)[:], (A.min, A.max)[s]))
-                op("V", vec(128), "ev%d" % s, "e16_%d" % s, lambda q, s=s: q.tensor_scalar(B("e16", s)[:], B("ev", s)[:], shift[s], None, A.add))
+                        op("V", vgat(128), "msk%d U%s %s%d" % (s, nm[1], ct, s), "%s%d" % (nm, s), lambda q, s=s, tab=tab, lo=lo, ct=ct: q.tensor_tensor(B("pp", s)[:, lo:lo + 128], tab[:].indirect(B(ct, s)[:]), B("msk", s)[:], A.mult), after=aft)
+                op("P", mm(256), "NK4 ones I nt", "qb%d" % s, lambda q, s=s: mms(q, [
+                    (PB[s][:, 0:128], T.NK4[:], T.ones[:], True, False),
+                    (PB[s][:, 0:128], T.I[:], T.nt[:], False, False)]), bank=bkB(s))
+                op("P", mm(128), "pq%d BOh" % s, "qb%d" % s, lambda q, s=s: q.matmul(PB[s][:, 0:128], T.BOh[:], B("pp", s)[:, 128:256], False, True), bank=bkB(s))
+                fold(s, 1)
+                op("S", act(128), "qb%d" % s, "tt%d" % s, lambda q, s=s: q.activation(B("tt", s)[:], PB[s][:, 0:128], F.Abs), bank=bkB(s))
+                if h == 0:
+                    op("V", vec(128), z + " f0%d" % s, "vb%d" % s, lambda q, s=s: q.tensor_tensor(VB[s], W[s][:, zcol], F0[s], A.subtract), bank=7)
+                op("V", vec(8), "wp%d" % s, "%s%d" % (nt, s), lambda q, s=s, nt=nt: q.tensor_copy(B(nt, s)[:], PA[s][:, 384:392]), bank=bkA(s))
+                op("V", vgat(128), "%s%d tt%d %s" % (nt, s, s, eall), "e16_%d" % s, lambda q, s=s, nt=nt: q.tensor_tensor(B("e16", s)[:], T.E[:].indirect(B(nt, s)[:]), B("tt", s)[:], A.min))
                 gather(s)
                 scans(s)
-                op("S", 90 + 128 * c_g, "%s%d BN" % (nt, s), "bg%d" % s, lambda q, s=s, nt=nt: q.activation(B("bg", s)[:], T.BN[:].indirect(B(nt, s)[:]), F.Copy))
-                op("V", vgat(128), "%s%d tt%d %s" % (nt, s, s, eall), "v1%d" % s, lambda q, s=s, nt=nt: q.tensor_tensor(B("v1", s)[:], T.E[:].indirect(B(nt, s)[:]), B("tt", s)[:], A.subtract))
-                op("S", act(128), "v1%d" % s, "dm%d%d" % (s, h), lambda q, s=s, h=h: q.activation(B("dm", s)[:, 128 * h:128 * h + 128], B("v1", s)[:], F.Sign, bias=-1535.5))
-                half(s, B("bg", s)[:], "bg%d" % s, W[:, zcol[s]], z)
+                op("S", sgat(128), "%s%d BN" % (nt, s), "bg%d" % s, lambda q, s=s, nt=nt: q.activation(B("bg", s)[:], T.BN[:].indirect(B(nt, s)[:]), F.Copy))
+                op("S", act(128), "tt%d" % s, "rr%d" % s, lambda q, s=s: q.activation(B("rr", s)[:], B("tt", s)[:], F.Relu, bias=-float(M)))
+                op("S", sgat(128), "%s%d %s" % (nt, s, call), "cg%d" % s, lambda q, s=s, nt=nt: q.activation(B("cg", s)[:], T.CR[:].indirect(B(nt, s)[:]), F.Copy))
+                op("P", mm(256), "cg%d rr%d I nI" % (s, s), "dq%d" % s, lambda q, s=s: mms(q, [
+                    (PB[s][:, 128:256], T.nI[:], B("rr", s)[:], True, False),
+                    (PB[s][:, 128:256], T.I[:], B("cg", s)[:], False, True)]), bank=bkB(s))
+                op("S", act(128), "dq%d" % s, "dm%d%d" % (s, h), lambda q, s=s, h=h: q.activation(B("dm", s)[:, 128 * h:128 * h + 128], PB[s][:, 128:256], F.Relu), bank=bkB(s))
+                half(s, B("bg", s)[:], "bg%d" % s, W[s][:, zcol], z)
                 if h == HP - 1:
-                    op("S", 90 + 128 * c_g, "%s%d Wx" % (nt, s), "xw%d" % s, lambda q, s=s, nt=nt: q.activation(B("xw", s)[:], W[:, X0:G0].indirect(B(nt, s)[:]), F.Copy))
-                    op("P", mm(256), z + " xw%d I nI" % s, "df%d" % s, lambda q, s=s: mms(q, [
-                        (PA[s][:, 0:128], T.nI[:], B("xw", s)[:], True, False),
-                        (PA[s][:, 0:128], T.I[:], W[:, zcol[s]], False, True)]), bank=bkA(s))
+                    op("S", sgat(128), "%s%d Wx%d" % (nt, s, s), "xw%d" % s, lambda q, s=s, nt=nt: q.activation(B("xw", s)[:], W[s][:, X0:G0].indirect(B(nt, s)[:]), F.Copy))
+                    op("P", mm(128), "xw%d nI" % s, "df%d" % s, lambda q, s=s: q.matmul(PA[s][:, 0:128], T.nI[:], B("xw", s)[:], True, False), bank=bkA(s))
+                    op("P", mm(128), z + " I", "df%d" % s, lambda q, s=s: q.matmul(PA[s][:, 0:128], T.I[:], W[s][:, zcol], False, True), bank=bkA(s))
                     op("S", act(128), "df%d" % s, "da%d" % s, lambda q, s=s: q.activation(B("da", s)[:], PA[s][:, 0:128], F.Abs), bank=bkA(s))
-                    op("P", mm(640), "da%d dm%d0 dm%d1 dm%d2 hs%d BO BD BH" % (s, s, s, s, s), "qq%d" % s, lambda q, s=s: mms(q, [
+                    op("P", mm(512), "dm%d0 dm%d1 dm%d2 hs%d BD BH" % (s, s, s, s), "qq%d" % s, lambda q, s=s: mms(q, [
                         (PB[s][:, 0:128], T.BH[:], B("hs", s)[:], True, False),
                         (PB[s][:, 0:128], T.BD[:], B("dm", s)[:, 0:128], False, False),
                         (PB[s][:, 0:128], T.BD[:], B("dm", s)[:, 128:256], False, False),
-                        (PB[s][:, 0:128], T.BD[:], B("dm", s)[:, 256:384], False, False),
-                        (PB[s][:, 0:128], T.BO[:], B("da", s)[:], False, True)]), bank=bkB(s))
+                        (PB[s][:, 0:128], T.BD[:], B("dm", s)[:, 256:384], False, False)]), bank=bkB(s))
+                    op("P", mm(128), "da%d BO" % s, "qq%d" % s, lambda q, s=s: q.matmul(PB[s][:, 0:128], T.BO[:], B("da", s)[:], False, True), bank=bkB(s))
                     op("V", vec(128), "qq%d thr%d" % (s, t), "st%d" % s, lambda q, s=s: q.tensor_scalar(B("st", s)[:], PB[s][:, 0:128], T.thr[:, t:t + 1], None, A.is_le), bank=bkB(s))
-                    op("V", vec(128, two=True), "st%d d0%d" % (s, s), "sd%d" % s, lambda q, s=s: q.tensor_tensor(B("sd", s)[:], B("st", s)[:], B("d0", s)[:], A.mult))
-                    op("V", vec(128, two=True), "sd%d f0%d" % (s, s), "XN%d" % s, lambda q, s=s: q.tensor_tensor(T.XN[:, 128 * s:128 * s + 128], B("sd", s)[:], B("f0", s)[:], A.add))
-        if t < RO - 1:
+                    op("V", vec(128), "st%d vb%d" % (s, s), "sd%d" % s, lambda q, s=s: q.tensor_tensor(B("sd", s)[:], B("st", s)[:], VB[s], A.mult), bank=7)
+                    op("V", vec(128), "sd%d f0%d" % (s, s), "XN%d" % s, lambda q, s=s: q.tensor_tensor(T.XN[:, 128 * s:128 * s + 128], B("sd", s)[:], F0[s], A.add), bank=7)
+        ctx[0] = 0
+        if not last:
             op("V", vgat(128), "XN0 XN1 snd16", "XG%d" % t, lambda q: q.tensor_copy(T.XG[:, 128 * t:128 * t + 128], T.XN[:].indirect(T.snd16[:, 8 * cl:8 * cl + 8])))
-            op("R", 2000, "XG%d" % t, "sent%d" % t, lambda q: q.remote_dma(T.gl[:, 128 * t:128 * t + 128], T.XG[:, 128 * t:128 * t + 128], T.sem["ga%d" % t], T.sem["ls%d" % t], pid, rid, mask), sem=("ls%d" % t, bin(mask).count("1")))
-            op("X", 3500, "sent%d" % t, "gl%d" % t, None, sem=("ga%d" % t, bin(mask).count("1")))
+            op("R", 2000, "XG%d" % t, "sent%d" % t, lambda q: q.remote_dma(T.gl[:, 128 * t:128 * t + 128], T.XG[:, 128 * t:128 * t + 128], T.sem["ga%d" % t], T.sem["ls%d" % t], pid, rid, mask), sem=("ls%d" % t, neng))
+            op("X", EST["remote"], "sent%d" % t, "gl%d" % t, None, sem=("ga%d" % t, neng))
         for s in range(NS):
-            op("V", vec(128), "XN%d" % s, "Wx", lambda q, s=s: q.tensor_copy(W[:, xsl[s]], T.XN[:, 128 * s:128 * s + 128]))
+            op("V", vec(128, True), "XN%d" % s, "Wx0", lambda q, s=s: q.tensor_copy(T.W0[:, xsl[s]], T.XN[:, 128 * s:128 * s + 128]))
+            if not last:
+                op("S", act(128), "XN%d" % s, "Wx1", lambda q, s=s: q.activation(T.W1[:, xsl[s]], T.XN[:, 128 * s:128 * s + 128], F.Copy))
+        for s in range(NS):
+            ec = ecls(s, cl)
+            if last:
+                op("V", vec(128), ec, "oe%d" % s, lambda q, s=s: q.tensor_scalar(T.OE[:, csl[s]], T.E[:, csl[s]], -X0, None, A.add))
             op("V", vec(128, two=True), "hs%d st%d" % (s, s), "eu%d" % s, lambda q, s=s: q.tensor_tensor(B("eu", s)[:], B("hs", s)[:], B("st", s)[:], A.mult))
-            op("V", vec(128, two=True), "eu%d %s" % (s, ecls(s, cl)), ecls(s, cl), lambda q, s=s: q.tensor_tensor(T.E[:, csl[s]], T.E[:, csl[s]], B("eu", s)[:], A.add))
-            if t < RO - 1:
-                op("S", act(128), "st%d" % s, "rs%d junk%d" % (s, s), lambda q, s=s: q.activation(T.junk[:, 128 * s:128 * s + 128], B("st", s)[:], F.Copy, accum_out=T.rs[:, s:s + 1]))
-        if t < RO - 1:
+            if last:
+                op("V", vec(128, two=True), "eu%d" % s, "oe%d" % s, lambda q, s=s: q.tensor_tensor(T.OE[:, csl[s]], T.OE[:, csl[s]], B("eu", s)[:], A.add))
+                dma("D", 4000, "oe%d" % s, "ye%d" % s, T.ye[:, 512 * s:512 * s + 512], T.OE[:, 512 * s:512 * s + 512])
+                continue
+            op("V", vec(128, two=True), "eu%d %s" % (s, ec), ec, lambda q, s=s: q.tensor_tensor(T.E[:, csl[s]], T.E[:, csl[s]], B("eu", s)[:], A.add))
+            op("V", vec(128), ec, "C" + ec, lambda q, s=s: q.tensor_scalar(T.CR[:, csl[s]], T.E[:, csl[s]], float(S + X0), None, A.is_ge))
+            if t > 0:
+                op("V", vec(128), ec, "oe%d" % s, lambda q, s=s: q.tensor_scalar(T.OE[:, csl[s]], T.E[:, csl[s]], -X0, None, A.add))
+            op("S", act(128), "st%d" % s, "rs%d junk%d" % (s, s), lambda q, s=s: q.activation(T.junk[:, 128 * s:128 * s + 128], B("st", s)[:], F.Copy, accum_out=T.rs[:, s:s + 1]))
+        if not last:
             op("P", mm(512), "rs0 rs1 c_os", "rp", lambda q: q.matmul(T.bk1[:, 0:2], T.c_os[:], T.rs[:], True, True), bank=1)
             op("V", vec(2), "rp", "rsum", lambda q: q.tensor_reduce(T.rsum[:, 0:1], T.bk1[:, 0:2], AxisListType.X, A.add), bank=1)
             op("V", vec(1), "rsum", "rint", lambda q: q.tensor_copy(T.rint[:, 0:1], T.rsum[:, 0:1]))
             op("V", vec(1), "rint", "rand", lambda q: q.tensor_scalar(T.rand[:, 0:1], T.rint[:, 0:1], 31, None, A.bitwise_and))
             op("V", vec(1), "rand thb", "thr%d" % (t + 1), lambda q: q.tensor_tensor(T.thr[:, t + 1:t + 2], T.thr[:, t + 1:t + 2], T.rand[:, 0:1], A.add))
-            op("V", vec(128, True), "gl%d" % t, "Wg", lambda q: q.tensor_copy(W[:, G0 + 128 * cl:G0 + 128 * cl + 128], T.gl[:, 128 * t:128 * t + 128]))
+            gs = slice(G0 + 128 * cl, G0 + 128 * cl + 128)
+            op("V", vec(128, True), "gl%d" % t, "Wg0", lambda q: q.tensor_copy(T.W0[:, gs], T.gl[:, 128 * t:128 * t + 128]))
+            op("S", act(128), "gl%d" % t, "Wg1", lambda q: q.activation(T.W1[:, gs], T.gl[:, 128 * t:128 * t + 128], F.Copy))
 
     for t in range(RO):
         one_round(t)
     for s in range(NS):
-        dma("D", 4000, " ".join(ecls(s, c) for c in range(4)), "oe%d" % s, T.ye[:, 512 * s:512 * s + 512], T.E[:, 512 * s:512 * s + 512])
-        dma("D", 4000, "Wx", "ox%d" % s, T.yx[:, 512 * s:512 * s + 512], W[:, X0 + 512 * s:X0 + 512 * s + 512])
+        dma("D", 4000, "Wx0", "yx%d" % s, T.yx[:, 512 * s:512 * s + 512], T.W0[:, X0 + 512 * s:X0 + 512 * s + 512])
     return ops
 
 
-QUEUE = {"V": "V", "S": "S", "P": "P", "G": "G", "R": "G", "D": "D", "X": "X"}
-WAKE = 80.0
+QUEUE = {"V": "V", "S": "S", "P": "P", "G": "G", "R": "G", "D": "D", "DS": "S", "X": "X"}
 
 
 def analyse(ops):
@@ -353,6 +413,8 @@ def analyse(ops):
         for x in o["r"]:
             if x in lastw:
                 d.add(lastw[x])
+        for x in o["after"]:
+            q.add(lastw[x])
         for x in o["w"]:
             prev = set(readers.get(x, ()))
             if x in lastw:
@@ -377,6 +439,7 @@ def analyse(ops):
 
 def schedule(ops, deps, order):
     n = len(ops)
+    wake = EST["wake"]
     succ = [[] for _ in range(n)]
     left = [0] * n
     for i in range(n):
@@ -385,25 +448,32 @@ def schedule(ops, deps, order):
             left[i] += 1
     prio = [0.0] * n
     for i in range(n - 1, -1, -1):
-        prio[i] = ops[i]["cost"] + max([prio[j] + WAKE for j in succ[i]] + [0.0])
+        prio[i] = ops[i]["cost"] + max([prio[j] + wake for j in succ[i]] + [0.0])
+    for i in range(n):
+        if ops[i]["s"] == 0:
+            prio[i] += EST["bias"]
     free, fin, ready = {}, [0.0] * n, [0.0] * n
     avail = [i for i in range(n) if left[i] == 0]
     seq = []
     busy = {}
+    look = EST["look"]
     while avail:
+        sts = [(max(ready[i], free.get(QUEUE[ops[i]["eng"]], 0.0)), i) for i in avail]
+        first = min(sts)
+        qf = QUEUE[ops[first[1]]["eng"]]
         best = None
-        for i in avail:
-            st = max(ready[i], free.get(QUEUE[ops[i]["eng"]], 0.0))
-            key = (st, -prio[i], i)
-            if best is None or key < best:
-                best = key
-        st, _, i = best
+        for st, i in sts:
+            if st <= first[0] + look and QUEUE[ops[i]["eng"]] == qf:
+                key = (-prio[i] + 3.0 * (st - first[0]), i)
+                if best is None or key < best[0]:
+                    best = (key, st, i)
+        _, st, i = best
         avail.remove(i)
         seq.append(i)
         e, c = ops[i]["eng"], ops[i]["cost"]
         fin[i] = st + c
-        if e == "D":
-            free["D"] = st + 60
+        if e in ("D", "DS"):
+            free[QUEUE[e]] = st + 60
         elif e == "R":
             free["G"] = st + 1000
         elif e != "X":
@@ -411,7 +481,7 @@ def schedule(ops, deps, order):
         busy[e] = busy.get(e, 0.0) + c
         for j in succ[i]:
             left[j] -= 1
-            ready[j] = max(ready[j], fin[i] + (WAKE if i in deps[j] else 0.0))
+            ready[j] = max(ready[j], fin[i] + (wake if i in deps[j] else 0.0))
             if left[j] == 0:
                 avail.append(j)
     return seq, fin, busy
@@ -465,12 +535,12 @@ def rank_program(g, core, T, topo):
             r.then_inc(T.sem["q" + q], 1)
         else:
             o["done"] = o["sem"]
-            if o["eng"] == "D":
+            if o["eng"] in ("D", "DS"):
                 r.then_inc(T.sem[o["sem"][0]], 16)
         after[i] = dict(kn)
         after[i][o["done"][0]] = o["done"][1]
     for q in ("V", "S", "P", "G"):
         g.wait_ge(T.sem["q" + q], count[q])
     for o in ops:
-        if o["eng"] in ("D", "R") and known["G"].get(o["sem"][0], 0) < o["sem"][1]:
+        if o["eng"] in ("D", "DS", "R") and known["G"].get(o["sem"][0], 0) < o["sem"][1]:
             g.wait_ge(T.sem[o["sem"][0]], o["sem"][1])

from concourse.mybir import AluOpType, AxisListType, ActivationFunctionType
A = AluOpType
F = ActivationFunctionType

S = 1536
NS, M = 2, 128
PIECES = [(0, 96, "S"), (96, 128, "V")]
CH = len(PIECES)
RO, HP = 5, 3
X0, G0, Y0, WE = 128, 1152, 1664, 3200
CMOD = 201326592.0
CINT = 8388608.0
HB = 1536.0
QOFF = -1024.0 * HB
CRND = 12582912.0
DV = (True, True)

SCRATCH = {
    "W0": ("sbuf", [128, WE], "bfloat16"),
    "W1": ("sbuf", [128, WE], "bfloat16"),
    "enti": ("sbuf", [128, 1024], "int32"),
    "E": ("sbuf", [128, 1024], "float32"),
    "OE": ("sbuf", [128, 1024], "float32"),
    "CR": ("sbuf", [128, 1024], "bfloat16"),
    "hI": ("sbuf", [128, 128], "bfloat16"),
    "usri": ("sbuf", [128, 1024], "int32"),
    "Uw": ("sbuf", [128, 1024], "int32"),
    "Uq": ("sbuf", [128, 1024], "int32"),
    "BN": ("sbuf", [128, 1024], "bfloat16"),
    "sndi": ("sbuf", [128, 32], "int32"),
    "snd16": ("sbuf", [128, 32], "uint16"),
    "gi16": ("sbuf", [128, 32], "uint16"),
    "thi": ("sbuf", [8, 5], "int32"),
    "thf": ("sbuf", [8, 5], "float32"),
    "thr": ("sbuf", [128, 8], "float32"),
    "XGi": ("sbuf", [128, 512], "bfloat16"),
    "XG": ("sbuf", [128, 512], "bfloat16"),
    "gl": ("sbuf", [128, 512], "bfloat16"),
    "XN": ("sbuf", [128, 256], "bfloat16"),
    "rs": ("sbuf", [128, 2], "float32"),
    "rsum": ("sbuf", [128, 8], "float32"),
    "rint": ("sbuf", [128, 16], "int32"),
    "rand": ("sbuf", [128, 16], "int32"),
    "junk": ("sbuf", [128, 256], "bfloat16"),
    "c_one": ("sbuf", [128, 128], "float32"),
    "c_if": ("sbuf", [128, 128], "float32"),
    "c_t1": ("sbuf", [128, 128], "float32"),
    "c_bof": ("sbuf", [128, 128], "float32"),
    "c_os": ("sbuf", [128, 128], "float32"),
    "c_pi": ("sbuf", [128, 1], "int32"),
    "c_ki": ("sbuf", [128, 1], "int32"),
    "kcol": ("sbuf", [128, 1], "float32"),
    "nkcol": ("sbuf", [128, 1], "float32"),
    "k16": ("sbuf", [128, 1], "float32"),
    "c_cl": ("sbuf", [128, 8], "int32"),
    "clist": ("sbuf", [128, 8], "uint16"),
    "c_nb": ("sbuf", [128, 8], "int32"),
    "nbase": ("sbuf", [128, 8], "bfloat16"),
    "nt": ("sbuf", [128, 128], "bfloat16"),
    "ones": ("sbuf", [128, 128], "bfloat16"),
    "I": ("sbuf", [128, 128], "bfloat16"),
    "nI": ("sbuf", [128, 128], "bfloat16"),
    "n2I": ("sbuf", [128, 128], "bfloat16"),
    "bigI": ("sbuf", [128, 128], "bfloat16"),
    "NK": ("sbuf", [128, 128], "bfloat16"),
    "NK4": ("sbuf", [128, 128], "bfloat16"),
    "KD": ("sbuf", [128, 128], "bfloat16"),
    "BO": ("sbuf", [128, 128], "bfloat16"),
    "BD": ("sbuf", [128, 128], "bfloat16"),
    "BH": ("sbuf", [128, 128], "bfloat16"),
    "BG": ("sbuf", [128, 8], "bfloat16"),
    "BOh": ("sbuf", [128, 128], "float16"),
    "BO1": ("sbuf", [128, 128], "float16"),
    "c_rc": ("sbuf", [128, 256], "float32"),
    "DM": ("sbuf", [128, 256], "bfloat16"),
    "mk_mx": ("sbuf", [128, 2048], "bfloat16"),
    "mk_mn": ("sbuf", [128, 2048], "bfloat16"),
    "mk_ky": ("sbuf", [128, 128], "float32"),
    "ex8": ("sbuf", [8, 128], "float32"),
}
for _s in range(NS):
    for _n, _w, _d in (("e16", 128, "uint16"), ("src", 2048, "bfloat16"), ("ab", 2048, "bfloat16"),
                       ("mx", 2048, "bfloat16"), ("mn", 2048, "bfloat16"), ("key", 128, "float32"), ("r1", 128, "float32"),
                       ("hit", 128, "bfloat16"), ("hs", 128, "bfloat16"), ("pp", 256, "float16"), ("wl", 256, "float16"), ("lst", 16, "uint16"),
                       ("ta", 8, "uint16"), ("tb", 8, "uint16"), ("yv", 128, "bfloat16"), ("fa", 128, "float32"),
                       ("r16", 128, "bfloat16"), ("msk", 128, "bfloat16"), ("dv", 512, "bfloat16"),
                       ("tt", 128, "float32"), ("rr", 128, "bfloat16"), ("cg", 128, "bfloat16"),
                       ("dm", 384, "bfloat16"), ("bg", 128, "bfloat16"),
                       ("xw", 128, "bfloat16"), ("da", 128, "bfloat16"), ("st", 128, "bfloat16"), ("sd", 128, "bfloat16"),
                       ("eu", 128, "bfloat16")):
        SCRATCH["%s_%d" % (_n, _s)] = ("sbuf", [128, _w], _d)
for _b in range(8):
    SCRATCH["bk%d" % _b] = ("psum", [128, 512], "float32")

SEMAPHORES = ["qV", "qS", "qP", "qG", "gini", "lini"] + ["ga%d" % t for t in range(4)] + ["ls%d" % t for t in range(4)] + ["d%d" % i for i in range(24)]

CY = 0.83
EST = {"fv": 30.0, "fs": 70.0, "fp": 25.0, "c": 1.45, "sc": 3.5, "wake": 70.0, "bias": 0.0, "remote": 3500.0, "ld": 1.0, "look": 60.0}


def program(T, topo, core):
    ops = []
    c_g = EST["c"] * CY
    ctx = [0]

    def op(eng, cost, reads, writes, fn, bank=None, sem=None, after=""):
        ops.append(dict(eng=eng, cost=cost, r=reads.split(), w=writes.split(), fn=fn, bank=bank, sem=sem, s=ctx[0], after=after.split()))

    def vec(n, half=False, two=False):
        return EST["fv"] + max(64, n * (0.5 if half else 2 if two else 1)) * CY

    def vgat(n):
        return 50 + n * c_g

    def act(n):
        return EST["fs"] + n * CY

    def sgat(n):
        return 65 + n * c_g

    def mm(cy):
        return EST["fp"] + cy * CY

    B = lambda n, s: T["%s_%d" % (n, s)]
    dst = T.cores[(T.rank_of(core) - 1) % 4]
    rid, pid = topo.addr(dst)[0], topo.addr(dst)[1]
    mask, neng = topo.mask(core, dst), len(topo.engines(core, dst))
    W = (T.W0, T.W1)
    ld = EST["ld"]

    dn = [0]

    def dma(eng, cost, reads, writes, out, in_):
        name = "d%d" % dn[0]
        dn[0] += 1
        op(eng, cost, reads, writes, (lambda q, out=out, in_=in_: q.dma_start(out, in_)), sem=(name, 16))

    dma("D", 2500 * ld, "", "sndi", T.sndi[:], T.snd[:])
    dma("D", 3000 * ld, "", "Wx0", W[0][:, X0:G0], T.xa[:])
    dma("DS", 5500 * ld, "", "enti", T.enti[:], T.ent[:])
    dma("D", 7000 * ld, "", "Wy0", W[0][:, Y0:WE], T.yc[:])
    dma("DS", 8000 * ld, "", "Wx1", W[1][:, X0:G0], T.xa[:])
    dma("D", 9000 * ld, "", "Wy1", W[1][:, Y0:WE], T.yc[:])
    dma("DS", 10000 * ld, "", "BN", T.BN[:], T.bn[:])
    dma("D", 12000 * ld, "", "usri", T.usri[:], T.usr[:])
    dma("DS", 12000 * ld, "", "thi", T.thi[:], T.th[:])

    for c in range(4):
        op("V", vec(8), "sndi", "gi16%d" % c, lambda q, c=c: q.tensor_scalar(T.gi16[:, 8 * c:8 * c + 8], T.sndi[:, 8 * c:8 * c + 8], 4, c, A.mult, A.add))
    op("V", vgat(512), "gi160 gi161 gi162 gi163 Wx0", "XGi", lambda q: q.tensor_copy(T.XGi[:], W[0][:, X0:G0].indirect(T.gi16[:])))
    op("R", 2000, "XGi", "sent", lambda q: q.remote_dma(W[0][:, G0:Y0], T.XGi[:], T.sem["gini"], T.sem["lini"], pid, rid, mask), sem=("lini", neng))
    op("X", 5000, "sent", "Wg0", None, sem=("gini", neng))
    op("V", vec(512, True), "Wg0", "Wg1", lambda q: q.tensor_copy(W[1][:, G0:Y0], W[0][:, G0:Y0]))
    op("V", vec(32), "sndi", "snd16", lambda q: q.tensor_copy(T.snd16[:], T.sndi[:]))

    op("V", vec(128), "", "c_one", lambda q: q.memset(T.c_one[:], 1.0))
    op("V", vec(128), "", "ones", lambda q: q.memset(T.ones[:], 1.0))
    op("V", vec(128), "", "c_os", lambda q: q.memset(T.c_os[:], 0.0625))
    op("V", vec(128), "", "za0", lambda q: q.memset(W[0][:, 0:X0], 0.0))
    op("V", vec(128), "", "za1", lambda q: q.memset(W[1][:, 0:X0], 0.0))
    op("V", vec(1024, True), "", "mk_mx", lambda q: q.memset(T.mk_mx[:], 255.0))
    op("V", vec(64), "", "mk_mx", lambda q: q.memset(T.mk_mx[:, 0:2048:16], 0.0))
    op("V", vec(1024, True), "", "mk_mn", lambda q: q.memset(T.mk_mn[:], 0.0))
    op("V", vec(64), "", "mk_mn", lambda q: q.memset(T.mk_mn[:, 0:2048:16], 255.0))
    op("V", vec(128), "", "mk_ky", lambda q: q.memset(T.mk_ky[:], 0.0))
    op("V", vec(64), "", "mk_ky", lambda q: q.memset(T.mk_ky[:, 0:128:16], 131071.0))
    op("G", 400, "c_one", "c_if", lambda q: q.affine_select(T.c_if[:], T.c_one[:], [[-1, 128]], A.is_equal, 0.0, 0, 1))
    op("G", 400, "c_one", "c_t1", lambda q: q.affine_select(T.c_t1[:], T.c_one[:], [[-16, 8], [0, 16]], A.is_ge, 0.0, 0, 1))
    op("G", 400, "c_t1", "c_bof", lambda q: q.affine_select(T.c_bof[:], T.c_t1[:], [[16, 8], [0, 16]], A.is_ge, 0.0, 15, -1))
    op("G", 200, "", "c_pi", lambda q: q.iota(T.c_pi[:], [[0, 1]], 0, 1))
    op("G", 200, "", "c_cl", lambda q: q.iota(T.c_cl[:], [[16, 8]], 15, 0))
    op("G", 200, "", "c_nb", lambda q: q.iota(T.c_nb[:], [[256, 8]], 0, 0))
    op("G", 400, "", "nt", lambda q: q.iota(T.nt[:], [[1, 128]], 0, 0, allow_small_or_imprecise_dtypes=True))
    op("G", 400, "c_one", "ex8", lambda q: q.affine_select(T.ex8[:], T.c_one[0:8, :], [[-1, 8], [0, 16]], A.is_equal, 0.0, 0, 1))
    op("V", vec(1), "c_pi", "c_ki", lambda q: q.tensor_scalar(T.c_ki[:], T.c_pi[:], 15, None, A.bitwise_and))
    op("V", vec(1), "c_ki", "kcol", lambda q: q.tensor_copy(T.kcol[:], T.c_ki[:]))
    op("V", vec(1), "kcol", "nkcol", lambda q: q.tensor_scalar(T.nkcol[:], T.kcol[:], -1.0, None, A.mult))
    op("V", vec(1), "kcol", "k16", lambda q: q.tensor_scalar(T.k16[:], T.kcol[:], 16.0, None, A.mult))
    op("V", vec(8), "c_cl", "clist", lambda q: q.tensor_copy(T.clist[:], T.c_cl[:]))
    op("V", vec(8), "c_nb k16", "nbase", lambda q: q.tensor_scalar(T.nbase[:], T.c_nb[:], T.k16[:], None, A.add))
    op("V", vec(128), "c_if", "I", lambda q: q.tensor_copy(T.I[:], T.c_if[:]))
    op("V", vec(128), "c_if", "nI", lambda q: q.tensor_scalar(T.nI[:], T.c_if[:], -1.0, None, A.mult))
    op("V", vec(128), "c_if", "n2I", lambda q: q.tensor_scalar(T.n2I[:], T.c_if[:], -2.0, None, A.mult))
    op("V", vec(128), "c_if", "hI", lambda q: q.tensor_scalar(T.hI[:], T.c_if[:], -0.5, None, A.mult))
    op("V", vec(128), "c_if", "bigI", lambda q: q.tensor_scalar(T.bigI[:], T.c_if[:], 131072.0, None, A.mult))
    op("V", vec(128), "c_if nkcol", "NK", lambda q: q.tensor_scalar(T.NK[:], T.c_if[:], T.nkcol[:], None, A.mult))
    op("V", vec(128), "c_if nkcol", "NK4", lambda q: q.tensor_scalar(T.NK4[:], T.c_if[:], T.nkcol[:], 4096.0, A.mult, A.mult))
    op("V", vec(128), "c_if kcol", "KD", lambda q: q.tensor_scalar(T.KD[:], T.c_if[:], T.kcol[:], None, A.mult))
    op("V", vec(128), "c_bof", "BO", lambda q: q.tensor_copy(T.BO[:], T.c_bof[:]))
    op("V", vec(128), "c_bof", "BD", lambda q: q.tensor_scalar(T.BD[:], T.c_bof[:], -8192.0, None, A.mult))
    op("V", vec(128), "c_bof", "BH", lambda q: q.tensor_scalar(T.BH[:], T.c_bof[:], -1024.0, None, A.mult))
    op("V", vec(8), "c_bof", "BG", lambda q: q.tensor_scalar(T.BG[:], T.c_bof[:, 0:128:16], 16.0, None, A.mult))
    op("V", vec(128), "c_bof", "BOh", lambda q: q.tensor_scalar(T.BOh[:], T.c_bof[:], 4096.0, None, A.mult))
    op("V", vec(128), "c_bof", "BO1", lambda q: q.tensor_copy(T.BO1[:], T.c_bof[:]))
    op("G", 600, "", "c_rc", lambda q: q.iota(T.c_rc[:], [[0, 16], [1, 16]], 0, 0, allow_small_or_imprecise_dtypes=True))
    op("V", vec(256), "c_rc kcol", "DM", lambda q: q.tensor_scalar(T.DM[:], T.c_rc[:], T.kcol[:], None, A.is_equal))
    op("V", vec(5), "thi", "thf", lambda q: q.tensor_copy(T.thf[:], T.thi[:]))
    op("P", mm(512), "thf ex8", "ps_th", lambda q: q.matmul(T.bk0[:, 0:5], T.ex8[:], T.thf[:], True, True), bank=0)
    op("V", vec(5), "ps_th", "thb thr0", lambda q: q.tensor_scalar(T.thr[:, 0:5], T.bk0[:, 0:5], QOFF, None, A.add), bank=0)

    ecls = lambda s, cl: "E%d%d" % (s, cl)
    eall = " ".join(ecls(s, cl) for s in range(NS) for cl in range(4))
    for cl in range(4):
        for s in range(NS):
            sl = slice(512 * s + cl, 512 * s + 512, 4)
            op("V", vec(128), "enti", ecls(s, cl), lambda q, sl=sl: q.tensor_scalar(T.E[:, sl], T.enti[:, sl], X0, None, A.add))
            op("V", vec(128), "enti", "C" + ecls(s, cl), lambda q, sl=sl: q.tensor_scalar(T.CR[:, sl], T.enti[:, sl], S, None, A.is_ge))
    call = " ".join("C" + x for x in eall.split())
    op("V", vec(1024), "usri", "Uq", lambda q: q.tensor_scalar(T.Uq[:], T.usri[:], 15, None, A.bitwise_and))
    op("V", vec(1024), "usri", "Uw", lambda q: q.tensor_scalar(T.Uw[:], T.usri[:], 4, None, A.arith_shift_right))

    def mms(q, lst):
        r = None
        for a in lst:
            r = q.matmul(*a)
        return r

    def bkA(s): return 2 * s
    def bkB(s): return 2 * s + 1
    PA = (T.bk0, T.bk2)
    PB = (T.bk1, T.bk3)
    PJ = (T.bk4, T.bk5, T.bk6)
    F0 = (T.bk7[:, 0:128], T.bk7[:, 128:256])
    VB = (T.bk7[:, 256:384], T.bk7[:, 384:512])
    zcol = slice(0, X0)

    def gather(s):
        for c, (lo, hi, who) in enumerate(PIECES):
            n = 16 * (hi - lo)
            rd, wr = "e16_%d Wx%d Wg%d Wy%d za%d" % (s, s, s, s, s), "src%d%d" % (s, c)
            out, in_ = B("src", s)[:, 16 * lo:16 * hi], W[s][:, 0:WE].indirect(B("e16", s)[:, lo:hi])
            if who == "S":
                op("S", sgat(n), rd, wr, lambda q, out=out, in_=in_: q.activation(out, in_, F.Copy))
            else:
                op("V", vgat(n), rd, wr, lambda q, out=out, in_=in_: q.tensor_copy(out, in_))

    def scans(s):
        for c, (lo, hi, who) in enumerate(PIECES):
            n, sl = 16 * (hi - lo), slice(16 * lo, 16 * hi)
            op("V", vec(n, True), "src%d%d mk_mx" % (s, c), "mx%d%d" % (s, c),
               lambda q, s=s, sl=sl, n=n: q.tensor_tensor_scan(B("mx", s)[:, sl], T.mk_mx[:, 0:n], B("src", s)[:, sl], 0.0, A.min, A.max))
            op("V", vec(n, True), "src%d%d mk_mn" % (s, c), "mn%d%d" % (s, c),
               lambda q, s=s, sl=sl, n=n: q.tensor_tensor_scan(B("mn", s)[:, sl], T.mk_mn[:, 0:n], B("src", s)[:, sl], 255.0, A.max, A.min))

    def half(s, bsrc, btok, out, otok, bank=None):
        op("P", mm(256), "n2I hI ones " + btok, "h%d" % s, lambda q, s=s: mms(q, [
            (PA[s][:, 0:128], T.hI[:], T.ones[:], True, False),
            (PA[s][:, 0:128], T.n2I[:], bsrc, False, False)]), bank=bkA(s))
        op("P", mm(128), "I " + " ".join("mx%d%d" % (s, c) for c in range(CH)), "h%d" % s, lambda q, s=s: q.matmul(PA[s][:, 0:128], T.I[:], B("mx", s)[:, 15:2048:16], False, False), bank=bkA(s))
        op("P", mm(128), "I " + " ".join("mn%d%d" % (s, c) for c in range(CH)), "h%d" % s, lambda q, s=s: q.matmul(PA[s][:, 0:128], T.I[:], B("mn", s)[:, 15:2048:16], False, True), bank=bkA(s))
        if bank is not None:
            op("S", act(128), "h%d" % s, "fa%d" % s, lambda q, s=s: q.activation(B("fa", s)[:], PA[s][:, 0:128], F.Abs, scale=0.5), bank=bkA(s))
            op("V", vec(128), "fa%d" % s, otok, lambda q, s=s: q.tensor_scalar(out, B("fa", s)[:], CINT, CINT, A.add, A.subtract), bank=bank)
        else:
            op("S", act(128), "h%d" % s, "fa%d" % s, lambda q, s=s: q.activation(B("fa", s)[:], PA[s][:, 0:128], F.Identity, bias=CRND, scale=0.5), bank=bkA(s))
            op("S", act(128), "fa%d" % s, otok, lambda q, s=s: q.activation(out, B("fa", s)[:], F.Abs, bias=-CRND))

    def fold(s, k):
        rd = ("pw%d" % s, "pw%d pq%d" % (s, s))[k - 1]
        op("P", mm(128 * k), rd + " BO1", "wi%d" % s, lambda q, s=s: mms(q, [
            (PA[s][:, 128 + 128 * j:256 + 128 * j], B("pp", s)[:, 128 * j:128 * j + 128], T.BO1[:], True, True) for j in range(k)]), bank=bkA(s), after="qb%d" % s if k == 1 else "")
        op("V", vec(128 * k), "wi%d DM" % s, "wl%d" % s, lambda q, s=s: q.tensor_tensor(B("wl", s)[:, 0:128 * k], PA[s][:, 128:128 + 128 * k], T.DM[:, 0:128 * k], A.mult), bank=bkA(s))
        op("P", mm(64 * (2 * k - 1)), "wl%d BO1 I nbase" % s, "wp%d" % s, lambda q, s=s: mms(q, [
            (PA[s][:, 384:392], B("wl", s)[:, 0:128], T.BO1[:, 0:128:16], True, True)] + ([
                (PA[s][:, 392:400], B("wl", s)[:, 128:256], T.BO1[:, 0:128:16], True, False),
                (PA[s][:, 392:400], T.I[:], T.nbase[:], False, True)] if k == 2 else [])), bank=bkA(s))

    def one_round(t):
        cl = t % 4
        last = t == RO - 1
        csl = [slice(512 * s + cl, 512 * s + 512, 4) for s in range(NS)]
        xsl = [slice(X0 + 512 * s + cl, X0 + 512 * s + 512, 4) for s in range(NS)]
        for s in range(NS):
            ctx[0] = s
            ec = ecls(s, cl)
            op("V", vec(128), ec, "e16_%d" % s, lambda q, s=s: q.tensor_copy(B("e16", s)[:], T.E[:, csl[s]]))
            gather(s)
            sr = " ".join("src%d%d" % (s, c) for c in range(CH))
            op("P", mm(256), "ones KD C%s bigI" % ec, "ky%d" % s, lambda q, s=s: mms(q, [
                (PB[s][:, 0:128], T.ones[:], T.KD[:], True, False),
                (PB[s][:, 0:128], T.CR[:, csl[s]], T.bigI[:], False, False)]), bank=bkB(s))
            for b in (3, 0, 1, 2):
                out = slice(512 * b, 512 * b + 512)
                if b == 3 and DV[s]:
                    for k in range(4):
                        op("V", vec(128, two=True), sr + " Wx%d" % s, "dv%d%d" % (s, k), lambda q, s=s, k=k: q.tensor_tensor(
                            B("dv", s)[:, 128 * k:128 * k + 128], B("src", s)[:, 12 + k:2048:16], W[s][:, xsl[s]], A.subtract))
                    op("S", act(512), " ".join("dv%d%d" % (s, k) for k in range(4)), "ab%d%d" % (s, b), lambda q, s=s, out=out: q.activation(B("ab", s)[:, out], B("dv", s)[:], F.Abs))
                else:
                    j = b % 3
                    op("P", mm(1024), sr + " I nI Wx%d" % s, "j%d" % j, lambda q, s=s, b=b, j=j: mms(q, [
                        a for k in range(4) for a in (
                            (PJ[j][:, 128 * k:128 * k + 128], T.I[:], B("src", s)[:, 4 * b + k:2048:16], True, False),
                            (PJ[j][:, 128 * k:128 * k + 128], T.nI[:], W[s][:, xsl[s]], False, True))]), bank=4 + j)
                    op("S", act(512), "j%d" % j, "ab%d%d" % (s, b), lambda q, s=s, out=out, j=j: q.activation(B("ab", s)[:, out], PJ[j][:], F.Abs), bank=4 + j)
            for b in (0, 1, 3, 2):
                op("P", mm(256), "ab%d%d BG" % (s, b), "ky%d" % s, lambda q, s=s, b=b: mms(q, [
                    (PB[s][:, k:128:16], B("ab", s)[:, 128 * k:128 * k + 128], T.BG[:], False, k == 11) for k in range(4 * b, 4 * b + 4)]), bank=bkB(s))
            scans(s)
            half(s, T.BN[:, csl[s]], "BN", F0[s], "f0%d" % s, 7)
            op("S", act(128), "ky%d" % s, "key%d" % s, lambda q, s=s: q.activation(B("key", s)[:], PB[s][:, 0:128], F.Copy), bank=bkB(s))
            op("V", vec(128), "key%d mk_ky" % s, "r1%d" % s, lambda q, s=s: q.tensor_tensor_scan(B("r1", s)[:], T.mk_ky[:], B("key", s)[:], 131071.0, A.max, A.min))
            op("V", vgat(128), "r1%d key%d clist" % (s, s), "hit%d" % s, lambda q, s=s: q.tensor_tensor(B("hit", s)[:], B("r1", s)[:].indirect(T.clist[:]), B("key", s)[:], A.is_equal))
            op("P", mm(128), "hit%d I" % s, "ht%d" % s, lambda q, s=s: q.matmul(PB[s][:, 256:384], B("hit", s)[:], T.I[:], True, True), bank=bkB(s))
            op("V", vec(128), "ht%d %s" % (s, ec), "pw%d" % s, lambda q, s=s: q.tensor_tensor(B("pp", s)[:, 0:128], PB[s][:, 256:384], T.E[:, csl[s]], A.mult), bank=bkB(s))
            op("V", vec(128), "ht%d kcol" % s, "pq%d" % s, lambda q, s=s: q.tensor_scalar(B("pp", s)[:, 128:256], PB[s][:, 256:384], T.kcol[:], None, A.mult), bank=bkB(s))
            fold(s, 2)
            op("S", act(128), "ht%d" % s, "hs%d" % s, lambda q, s=s: q.activation(B("hs", s)[:], PB[s][:, 256:384], F.Copy, scale=HB), bank=bkB(s))
            op("V", vec(16), "wp%d" % s, "lst%d" % s, lambda q, s=s: q.tensor_copy(B("lst", s)[:], PA[s][:, 384:400]), bank=bkA(s))
            op("S", sgat(128), "lst%d Wy%d Wg%d" % (s, s, s), "yv%d" % s, lambda q, s=s: q.activation(B("yv", s)[:], W[s][:, Y0 - X0:WE].indirect(B("lst", s)[:, 0:8]), F.Copy))
            op("V", 50 + 128 * EST["sc"] * CY, "lst%d yv%d" % (s, s), sr, lambda q, s=s: q.tensor_copy(B("src", s)[:].indirect(B("lst", s)[:, 8:16]), B("yv", s)[:]))
            scans(s)
            half(s, T.BN[:, csl[s]], "BN", W[s][:, zcol], "za%d" % s)
        for h in range(HP):
            for s in range(NS):
                ctx[0] = s
                z = "za%d" % s
                nt, ct = ("ta", "tb")[h % 2], ("tb", "ta")[h % 2]
                op("P", mm(128), "NK ones", "s%d" % s, lambda q, s=s: q.matmul(PA[s][:, 0:128], T.NK[:], T.ones[:], True, False), bank=bkA(s))
                op("P", mm(128), z + " BO", "s%d" % s, lambda q, s=s: q.matmul(PA[s][:, 0:128], T.BO[:], W[s][:, zcol], False, True), bank=bkA(s))
                op("V", vec(128), "s%d" % s, "r16%d" % s, lambda q, s=s: q.tensor_scalar(B("r16", s)[:], PA[s][:, 0:128], CMOD, CMOD, A.add, A.subtract), bank=bkA(s))
                if h == 0:
                    op("V", vec(128), "s%d r16%d" % (s, s), "vb%d" % s, lambda q, s=s: q.tensor_tensor(VB[s], PA[s][:, 0:128], B("r16", s)[:], A.is_equal), bank=bkA(s))
                else:
                    op("V", vec(128), "s%d r16%d" % (s, s), "msk%d" % s, lambda q, s=s: q.tensor_tensor(B("msk", s)[:], PA[s][:, 0:128], B("r16", s)[:], A.is_equal), bank=bkA(s))
                for nm, tab, lo, aft in (("pq", T.Uq, 128, ""), ("pw", T.Uw, 0, "pq%d" % s)):
                    if h == 0:
                        op("V", vec(128), "vb%d U%s" % (s, nm[1]), "%s%d" % (nm, s), lambda q, s=s, tab=tab, lo=lo: q.tensor_tensor(B("pp", s)[:, lo:lo + 128], tab[:, csl[s]], VB[s], A.mult), bank=7, after=aft)
                    else:
                        op("V", vgat(128), "msk%d U%s %s%d" % (s, nm[1], ct, s), "%s%d" % (nm, s), lambda q, s=s, tab=tab, lo=lo, ct=ct: q.tensor_tensor(B("pp", s)[:, lo:lo + 128], tab[:].indirect(B(ct, s)[:]), B("msk", s)[:], A.mult), after=aft)
                op("P", mm(256), "NK4 ones I nt", "qb%d" % s, lambda q, s=s: mms(q, [
                    (PB[s][:, 0:128], T.NK4[:], T.ones[:], True, False),
                    (PB[s][:, 0:128], T.I[:], T.nt[:], False, False)]), bank=bkB(s))
                op("P", mm(128), "pq%d BOh" % s, "qb%d" % s, lambda q, s=s: q.matmul(PB[s][:, 0:128], T.BOh[:], B("pp", s)[:, 128:256], False, True), bank=bkB(s))
                fold(s, 1)
                op("S", act(128), "qb%d" % s, "tt%d" % s, lambda q, s=s: q.activation(B("tt", s)[:], PB[s][:, 0:128], F.Abs), bank=bkB(s))
                if h == 0:
                    op("V", vec(128), z + " f0%d" % s, "vb%d" % s, lambda q, s=s: q.tensor_tensor(VB[s], W[s][:, zcol], F0[s], A.subtract), bank=7)
                op("V", vec(8), "wp%d" % s, "%s%d" % (nt, s), lambda q, s=s, nt=nt: q.tensor_copy(B(nt, s)[:], PA[s][:, 384:392]), bank=bkA(s))
                op("V", vgat(128), "%s%d tt%d %s" % (nt, s, s, eall), "e16_%d" % s, lambda q, s=s, nt=nt: q.tensor_tensor(B("e16", s)[:], T.E[:].indirect(B(nt, s)[:]), B("tt", s)[:], A.min))
                gather(s)
                scans(s)
                op("S", sgat(128), "%s%d BN" % (nt, s), "bg%d" % s, lambda q, s=s, nt=nt: q.activation(B("bg", s)[:], T.BN[:].indirect(B(nt, s)[:]), F.Copy))
                op("S", act(128), "tt%d" % s, "rr%d" % s, lambda q, s=s: q.activation(B("rr", s)[:], B("tt", s)[:], F.Relu, bias=-float(M)))
                op("S", sgat(128), "%s%d %s" % (nt, s, call), "cg%d" % s, lambda q, s=s, nt=nt: q.activation(B("cg", s)[:], T.CR[:].indirect(B(nt, s)[:]), F.Copy))
                op("P", mm(256), "cg%d rr%d I nI" % (s, s), "dq%d" % s, lambda q, s=s: mms(q, [
                    (PB[s][:, 128:256], T.nI[:], B("rr", s)[:], True, False),
                    (PB[s][:, 128:256], T.I[:], B("cg", s)[:], False, True)]), bank=bkB(s))
                op("S", act(128), "dq%d" % s, "dm%d%d" % (s, h), lambda q, s=s, h=h: q.activation(B("dm", s)[:, 128 * h:128 * h + 128], PB[s][:, 128:256], F.Relu), bank=bkB(s))
                half(s, B("bg", s)[:], "bg%d" % s, W[s][:, zcol], z)
                if h == HP - 1:
                    op("S", sgat(128), "%s%d Wx%d" % (nt, s, s), "xw%d" % s, lambda q, s=s, nt=nt: q.activation(B("xw", s)[:], W[s][:, X0:G0].indirect(B(nt, s)[:]), F.Copy))
                    op("P", mm(128), "xw%d nI" % s, "df%d" % s, lambda q, s=s: q.matmul(PA[s][:, 0:128], T.nI[:], B("xw", s)[:], True, False), bank=bkA(s))
                    op("P", mm(128), z + " I", "df%d" % s, lambda q, s=s: q.matmul(PA[s][:, 0:128], T.I[:], W[s][:, zcol], False, True), bank=bkA(s))
                    op("S", act(128), "df%d" % s, "da%d" % s, lambda q, s=s: q.activation(B("da", s)[:], PA[s][:, 0:128], F.Abs), bank=bkA(s))
                    op("P", mm(512), "dm%d0 dm%d1 dm%d2 hs%d BD BH" % (s, s, s, s), "qq%d" % s, lambda q, s=s: mms(q, [
                        (PB[s][:, 0:128], T.BH[:], B("hs", s)[:], True, False),
                        (PB[s][:, 0:128], T.BD[:], B("dm", s)[:, 0:128], False, False),
                        (PB[s][:, 0:128], T.BD[:], B("dm", s)[:, 128:256], False, False),
                        (PB[s][:, 0:128], T.BD[:], B("dm", s)[:, 256:384], False, False)]), bank=bkB(s))
                    op("P", mm(128), "da%d BO" % s, "qq%d" % s, lambda q, s=s: q.matmul(PB[s][:, 0:128], T.BO[:], B("da", s)[:], False, True), bank=bkB(s))
                    op("V", vec(128), "qq%d thr%d" % (s, t), "st%d" % s, lambda q, s=s: q.tensor_scalar(B("st", s)[:], PB[s][:, 0:128], T.thr[:, t:t + 1], None, A.is_le), bank=bkB(s))
                    op("V", vec(128), "st%d vb%d" % (s, s), "sd%d" % s, lambda q, s=s: q.tensor_tensor(B("sd", s)[:], B("st", s)[:], VB[s], A.mult), bank=7)
                    op("V", vec(128), "sd%d f0%d" % (s, s), "XN%d" % s, lambda q, s=s: q.tensor_tensor(T.XN[:, 128 * s:128 * s + 128], B("sd", s)[:], F0[s], A.add), bank=7)
        ctx[0] = 0
        if not last:
            op("V", vgat(128), "XN0 XN1 snd16", "XG%d" % t, lambda q: q.tensor_copy(T.XG[:, 128 * t:128 * t + 128], T.XN[:].indirect(T.snd16[:, 8 * cl:8 * cl + 8])))
            op("R", 2000, "XG%d" % t, "sent%d" % t, lambda q: q.remote_dma(T.gl[:, 128 * t:128 * t + 128], T.XG[:, 128 * t:128 * t + 128], T.sem["ga%d" % t], T.sem["ls%d" % t], pid, rid, mask), sem=("ls%d" % t, neng))
            op("X", EST["remote"], "sent%d" % t, "gl%d" % t, None, sem=("ga%d" % t, neng))
        for s in range(NS):
            op("V", vec(128, True), "XN%d" % s, "Wx0", lambda q, s=s: q.tensor_copy(T.W0[:, xsl[s]], T.XN[:, 128 * s:128 * s + 128]))
            if not last:
                op("S", act(128), "XN%d" % s, "Wx1", lambda q, s=s: q.activation(T.W1[:, xsl[s]], T.XN[:, 128 * s:128 * s + 128], F.Copy))
        for s in range(NS):
            ec = ecls(s, cl)
            if last:
                op("V", vec(128), ec, "oe%d" % s, lambda q, s=s: q.tensor_scalar(T.OE[:, csl[s]], T.E[:, csl[s]], -X0, None, A.add))
            op("V", vec(128, two=True), "hs%d st%d" % (s, s), "eu%d" % s, lambda q, s=s: q.tensor_tensor(B("eu", s)[:], B("hs", s)[:], B("st", s)[:], A.mult))
            if last:
                op("V", vec(128, two=True), "eu%d" % s, "oe%d" % s, lambda q, s=s: q.tensor_tensor(T.OE[:, csl[s]], T.OE[:, csl[s]], B("eu", s)[:], A.add))
                dma("D", 4000, "oe%d" % s, "ye%d" % s, T.ye[:, 512 * s:512 * s + 512], T.OE[:, 512 * s:512 * s + 512])
                continue
            op("V", vec(128, two=True), "eu%d %s" % (s, ec), ec, lambda q, s=s: q.tensor_tensor(T.E[:, csl[s]], T.E[:, csl[s]], B("eu", s)[:], A.add))
            op("V", vec(128), ec, "C" + ec, lambda q, s=s: q.tensor_scalar(T.CR[:, csl[s]], T.E[:, csl[s]], float(S + X0), None, A.is_ge))
            if t > 0:
                op("V", vec(128), ec, "oe%d" % s, lambda q, s=s: q.tensor_scalar(T.OE[:, csl[s]], T.E[:, csl[s]], -X0, None, A.add))
            op("S", act(128), "st%d" % s, "rs%d junk%d" % (s, s), lambda q, s=s: q.activation(T.junk[:, 128 * s:128 * s + 128], B("st", s)[:], F.Copy, accum_out=T.rs[:, s:s + 1]))
        if not last:
            op("P", mm(512), "rs0 rs1 c_os", "rp", lambda q: q.matmul(T.bk1[:, 0:2], T.c_os[:], T.rs[:], True, True), bank=1)
            op("V", vec(2), "rp", "rsum", lambda q: q.tensor_reduce(T.rsum[:, 0:1], T.bk1[:, 0:2], AxisListType.X, A.add), bank=1)
            op("V", vec(1), "rsum", "rint", lambda q: q.tensor_copy(T.rint[:, 0:1], T.rsum[:, 0:1]))
            op("V", vec(1), "rint", "rand", lambda q: q.tensor_scalar(T.rand[:, 0:1], T.rint[:, 0:1], 31, None, A.bitwise_and))
            op("V", vec(1), "rand thb", "thr%d" % (t + 1), lambda q: q.tensor_tensor(T.thr[:, t + 1:t + 2], T.thr[:, t + 1:t + 2], T.rand[:, 0:1], A.add))
            gs = slice(G0 + 128 * cl, G0 + 128 * cl + 128)
            op("V", vec(128, True), "gl%d" % t, "Wg0", lambda q: q.tensor_copy(T.W0[:, gs], T.gl[:, 128 * t:128 * t + 128]))
            op("S", act(128), "gl%d" % t, "Wg1", lambda q: q.activation(T.W1[:, gs], T.gl[:, 128 * t:128 * t + 128], F.Copy))

    for t in range(RO):
        one_round(t)
    for s in range(NS):
        dma("D", 4000, "Wx0", "yx%d" % s, T.yx[:, 512 * s:512 * s + 512], T.W0[:, X0 + 512 * s:X0 + 512 * s + 512])
    return ops


QUEUE = {"V": "V", "S": "S", "P": "P", "G": "G", "R": "G", "D": "D", "DS": "S", "X": "X"}


def analyse(ops):
    lastw, readers, bank = {}, {}, {}
    deps, order = [], []
    for i, o in enumerate(ops):
        d, q = set(), set()
        for x in o["r"]:
            if x in lastw:
                d.add(lastw[x])
        for x in o["after"]:
            q.add(lastw[x])
        for x in o["w"]:
            prev = set(readers.get(x, ()))
            if x in lastw:
                prev.add(lastw[x])
            for p in prev:
                if p != i:
                    (q if o["eng"] == "P" and ops[p]["eng"] == "P" else d).add(p)
        if o["bank"] is not None and o["bank"] in bank:
            p = bank[o["bank"]]
            (q if ops[p]["eng"] == o["eng"] else d).add(p)
        for x in o["r"]:
            readers.setdefault(x, set()).add(i)
        for x in o["w"]:
            lastw[x] = i
            readers[x] = set()
        if o["bank"] is not None:
            bank[o["bank"]] = i
        deps.append(d)
        order.append(q)
    return deps, order


def schedule(ops, deps, order):
    n = len(ops)
    wake = EST["wake"]
    succ = [[] for _ in range(n)]
    left = [0] * n
    for i in range(n):
        for p in deps[i] | order[i]:
            succ[p].append(i)
            left[i] += 1
    prio = [0.0] * n
    for i in range(n - 1, -1, -1):
        prio[i] = ops[i]["cost"] + max([prio[j] + wake for j in succ[i]] + [0.0])
    for i in range(n):
        if ops[i]["s"] == 0:
            prio[i] += EST["bias"]
    free, fin, ready = {}, [0.0] * n, [0.0] * n
    avail = [i for i in range(n) if left[i] == 0]
    seq = []
    busy = {}
    look = EST["look"]
    while avail:
        sts = [(max(ready[i], free.get(QUEUE[ops[i]["eng"]], 0.0)), i) for i in avail]
        first = min(sts)
        qf = QUEUE[ops[first[1]]["eng"]]
        best = None
        for st, i in sts:
            if st <= first[0] + look and QUEUE[ops[i]["eng"]] == qf:
                key = (-prio[i] + 3.0 * (st - first[0]), i)
                if best is None or key < best[0]:
                    best = (key, st, i)
        _, st, i = best
        avail.remove(i)
        seq.append(i)
        e, c = ops[i]["eng"], ops[i]["cost"]
        fin[i] = st + c
        if e in ("D", "DS"):
            free[QUEUE[e]] = st + 60
        elif e == "R":
            free["G"] = st + 1000
        elif e != "X":
            free[QUEUE[e]] = st + c
        busy[e] = busy.get(e, 0.0) + c
        for j in succ[i]:
            left[j] -= 1
            ready[j] = max(ready[j], fin[i] + (wake if i in deps[j] else 0.0))
            if left[j] == 0:
                avail.append(j)
    return seq, fin, busy


PLAN = {}


def rank_program(g, core, T, topo):
    rank = T.rank_of(core)
    if rank is None:
        return
    ops = program(T, topo, core)
    if "seq" not in PLAN:
        deps, order = analyse(ops)
        PLAN["deps"], PLAN["seq"] = deps, schedule(ops, deps, order)[0]
    deps, seq = PLAN["deps"], PLAN["seq"]
    qs = {"V": g.vector, "S": g.scalar, "P": g.tensor, "G": g, "D": g.sync}
    count = {"V": 0, "S": 0, "P": 0, "G": 0}
    known = {q: {} for q in qs}
    after = {}
    for i in seq:
        o = ops[i]
        if o["eng"] == "X":
            o["done"] = o["sem"]
            after[i] = {o["sem"][0]: o["sem"][1]}
            continue
        q = QUEUE[o["eng"]]
        kn = known[q]
        need = {}
        for d in deps[i]:
            nm, v = ops[d]["done"]
            if kn.get(nm, 0) < v:
                need[nm] = max(need.get(nm, 0), v)
        for nm, v in need.items():
            implied = False
            for d in deps[i]:
                dn, dv = ops[d]["done"]
                if dn != nm and need.get(dn, 0) >= dv and after[d].get(nm, 0) >= v:
                    implied = True
            if not implied:
                qs[q].wait_ge(T.sem[nm], v)
        for d in deps[i]:
            for nm, v in after[d].items():
                if kn.get(nm, 0) < v:
                    kn[nm] = v
        r = o["fn"](qs[q])
        if o["eng"] in count:
            count[q] += 1
            o["done"] = ("q" + q, count[q])
            r.then_inc(T.sem["q" + q], 1)
        else:
            o["done"] = o["sem"]
            if o["eng"] in ("D", "DS"):
                r.then_inc(T.sem[o["sem"][0]], 16)
        after[i] = dict(kn)
        after[i][o["done"][0]] = o["done"][1]
    for q in ("V", "S", "P", "G"):
        g.wait_ge(T.sem["q" + q], count[q])
    for o in ops:
        if o["eng"] in ("D", "DS", "R") and known["G"].get(o["sem"][0], 0) < o["sem"][1]:
            g.wait_ge(T.sem[o["sem"][0]], o["sem"][1])
